import numpy as np, ml_dtypes
CORES = [1,5,17,21,33,37,49,53]
N = 8
import mx_ref
BF = ml_dtypes.bfloat16
def pick(q, e):
    c = np.concatenate([q[0].reshape(128, -1, 4), np.zeros((128, 1, 4), np.uint8)], axis=1); s = np.concatenate([q[1], np.ones((16, 1), np.uint8)], axis=1)
    return (np.ascontiguousarray(c[:, e].reshape(128, -1)), np.ascontiguousarray(s[:, e]))
def join(*qs):
    return (np.concatenate([q[0] for q in qs], axis=1), np.concatenate([q[1] for q in qs], axis=1))
def put(q, e, v):
    c, s = q[0].reshape(128, -1, 4).copy(), q[1].copy(); c[:, e] = v[0].reshape(128, -1, 4); s[:, e] = v[1]
    return (c.reshape(128, -1), s)
def pk(c, s):
    return (np.ascontiguousarray(c), mx_ref.live(s))
def emit(q):
    return q[0], q[1]
def tile(rs):
    return np.stack(rs, axis=2).reshape(128, -1).astype(BF)
def cut(t, i, w=512):
    return t[:, w * i:w * i + w]
def f(rng, *shape):
    return mx_ref.flush((rng.standard_normal(shape, dtype=np.float32) * np.exp2(rng.integers(-2, 3, shape[:-1] + (1,)))).astype(BF))
def wide(rng, *shape, cols=0):
    v = rng.standard_normal(shape, dtype=np.float32) * np.exp2(rng.integers(-12, 13, shape)).astype(np.float32)
    if cols: v *= np.repeat(np.exp2(rng.integers(-cols, cols + 1, shape[:-2] + (1, shape[-1] // 4))) * (rng.random(shape[:-2] + (1, shape[-1] // 4)) > 0.0625), 4, axis=-1).astype(np.float32)
    return mx_ref.flush(v.astype(BF))
T, CAPP, CAPR = 128, 48, 32
def same(t):
    return np.stack([np.concatenate([t, np.zeros((128, 512 - t.shape[1]), BF)], axis=1)] * N)
def bf(t):
    return np.asarray(t, np.float32).astype(BF)
def sized(rng, *shape):
    return 1 + rng.random(shape)
def signs(rng, *shape):
    return 1 - 2 * rng.integers(0, 2, shape)
def setup_inputs(rng):
    return {"x": f(rng, N, 128, 4 * T), "rt": same(f(rng, 128, 4 * N)), "w": f(rng, N, 128, 2048), "u": same(f(rng, 128, 4)), "v": f(rng, N, 128, 512)}
def planted(rng, a, b, own=1.0, off=1.0, way=1):
    d = setup_inputs(rng)
    at = np.arange(128) // (128 // N)
    big, mid = at[None, :, None] == a[:, None, :], at[None, :, None] == b[:, None, :]
    k = np.where(big, 16.0, np.where(mid, 4.0, 1.0))[..., None]
    g = np.where((big | mid)[..., None], 1, signs(rng, N, 128, T, 4))
    d["x"] = bf(sized(rng, N, 128, T, 4) * k * g).reshape(N, 128, 4 * T)
    d["rt"] = same(bf(sized(rng, 128, N, 4) * (at[:, None] == np.arange(N))[..., None]).reshape(128, 4 * N))
    d["w"] = bf(sized(rng, N, 128, 2048) * signs(rng, N, 128, 2048) * np.where(at == np.arange(N)[:, None], own, off)[..., None])
    d["u"] = same(bf(way * sized(rng, 128, 4)))
    return d
def setup_inputs_crowd(rng):
    a, b = np.zeros((N, T), int), np.zeros((N, T), int)
    for s in range(N):
        h, k = (s + (0, 1, 1)[s % 3]) % N, (s + (1, 0, 2)[s % 3]) % N
        rest = rng.permutation(np.array([e for e in range(N) if e not in (h, k)]))
        m, n = rest[np.arange(T) % rest.size], rest[np.arange(1, T + 1) % rest.size]
        p = rng.permutation(T)
        p[:CAPP + 16] = np.sort(p[:CAPP + 16])
        m[:CAPP + 16] = h
        m[CAPP + 16:CAPP + 16 + CAPR] = k
        n[np.concatenate([np.arange(CAPP + 16 + CAPR, T), np.arange(CAPP)])[:CAPP - CAPR]] = k
        a[s, p], b[s, p] = m, n
    return planted(rng, a, b, own=2.0 ** -4, way=-2.0 ** 24)
def setup_inputs_second(rng):
    a, b = np.zeros((N, T), int), np.zeros((N, T), int)
    one, i = int(rng.integers(0, N)), np.arange(T)
    half, last = CAPP // 2, CAPP + CAPP // 2 + 16
    for s in range(N):
        g = rng.permutation(N)
        h, k, rest = g[0], g[1], g[2:]
        m, n = rest[i % rest.size], rest[(i + 1) % rest.size]
        if s == one:
            m[:] = h
            n = g[1 + i % (N - 1)]
        else:
            m[:last] = h
            n[half:last] = k
        turn = (i + rng.integers(0, 2)) % 2 == 1
        p = rng.permutation(T)
        p[:last] = np.sort(p[:last])
        a[s, p], b[s, p] = np.where(turn, m, n), np.where(turn, n, m)
    return planted(rng, a, b, own=2.0 ** 4, way=-1)
def setup_inputs_ties(rng):
    kind = np.stack([rng.permutation(T) % N for s in range(N)])
    e = rng.integers(2, N, (N, T))
    a = np.where(kind == 0, 0, e)
    b = np.where(kind == 0, e, np.where(kind == 1, 0, e ^ 1))
    d = planted(rng, a, b)
    d["rt"][:, :, 4:8] = d["rt"][:, :, :4]
    d["w"][1::2] = d["w"][::2]
    d["w"][:2, :, :4] = 0
    d["w"][1, 128 // N, 0] = BF(4)
    return d
def setup_inputs_zero(rng):
    a = rng.integers(0, N, (N, T))
    b = (a + rng.integers(1, N, (N, T))) % N
    d = planted(rng, a, b, way=-1)
    at, late = np.arange(128) // (128 // N), np.arange(128) % (128 // N) >= 128 // N // 2
    kind = np.stack([rng.permutation(T) % 4 for s in range(N)])
    low = (at[None, :, None] == a[:, None, :]) & (kind % 2 == 1)[:, None, :] | (at[None, :, None] == b[:, None, :]) & (kind >= 2)[:, None, :]
    t = d["x"].astype(np.float32).reshape(N, 128, T, 4)
    d["x"] = bf(np.where(late[None, :, None, None], np.abs(t) * np.where(low, -1, 1)[..., None], t)).reshape(N, 128, 4 * T)
    d["rt"] = bf(d["rt"].astype(np.float32) * ~late[None, :, None])
    d["w"] = bf(np.abs(d["w"].astype(np.float32)) * ((at == np.arange(N)[:, None]) & late)[..., None])
    return d
def setup_inputs_spread(rng):
    return {**setup_inputs(rng), "x": wide(rng, N, 128, 4 * T, cols=6)}
def check_inputs(d):
    b = []
    for k in ("x", "rt", "w", "u", "v"):
        t = np.abs(d[k].astype(np.float32))
        if not (np.isfinite(t).all() and ((t == 0) | (t >= 2.0 ** -30) & (t <= 2.0 ** 30)).all()): b.append("a value of " + k)
    for k, n in (("rt", N), ("u", 1)):
        t = d[k].astype(np.float32)
        if (t[:, :, 4 * n:] != 0).any(): b.append(k + " has numbers behind its first columns")
        if (t != t[:1]).any(): b.append(k + " isn't the same on all ranks")
    return b
def reference(x, rt, w, u, v):
    q, a, b = [], [], []
    for s in range(N):
        q.append(mx_ref.quantize(np.ascontiguousarray(x[s])))
        z = mx_ref.matmul(mx_ref.quantize(np.ascontiguousarray(rt[s])), q[s])[:N] + np.float32(0)
        o = np.argsort(-z, axis=0, kind="stable")
        a.append(o[0])
        b.append(o[1])
    took = [[np.flatnonzero((a[s] == e) | (b[s] == e))[:CAPP] for e in range(N)] for s in range(N)]
    good = np.full((N, N, T), -np.inf, np.float32)
    made = []
    for e in range(N):
        t = join(*[pick(q[s], np.concatenate([took[s][e], np.full(CAPP - took[s][e].size, -1)])) for s in range(N)])
        rs = [mx_ref.matmul(mx_ref.quantize(np.ascontiguousarray(cut(w[e], i))), t) for i in range(4)]
        made.append(mx_ref.quantize(tile([np.maximum(k, np.float32(0)) * np.float32(0.0625) for k in rs])))
        z = mx_ref.matmul(mx_ref.quantize(np.ascontiguousarray(u[e])), made[e])[0] + np.float32(0)
        for s in range(N): good[s, e, took[s][e]] = z[s * CAPP:s * CAPP + took[s][e].size]
    every = join(*made)
    oc, osc = np.zeros((N, 128, 4 * T), np.uint8), np.zeros((N, 16, T), np.uint8)
    wn, y = np.zeros((N, 1, T), np.float32), np.zeros((N, 128, T), np.float32)
    for s in range(N):
        ga, gb = good[s, a[s], np.arange(T)], good[s, b[s], np.arange(T)]
        win = np.where(ga >= gb, a[s], b[s])
        none = np.maximum(ga, gb) == -np.inf
        wn[s, 0] = np.where(none, -100, -1 - win)
        at = np.full(T, -1)
        for e in range(N):
            home = np.flatnonzero((win == e) & ~none)[:CAPR]
            wn[s, 0, home] = e
            at[home] = (e * N + s) * CAPP + np.searchsorted(took[s][e], home)
        z = pick(every, at)
        oc[s], osc[s] = emit(z)
        y[s] = mx_ref.matmul(mx_ref.quantize(np.ascontiguousarray(v[s])), z)
    return {"oc": oc, "osc": osc, "wn": wn, "y": y}

@@ -1,0 +1,443 @@
+from concourse.bass import DstId, RemoteDMATransfer
+from concourse.mybir import dt, AluOpType, AxisListType, ActivationFunctionType
+
+OP, ACT = AluOpType, ActivationFunctionType
+CAPP, CAPR = 48, 32
+LEAST = 128
+Z0 = LEAST - CAPP
+END = Z0 + 8 * CAPP
+FW = 144
+CUT = 96
+TW = 160
+BIG = 9e29
+BANK = 512
+
+SCRATCH = {"ps": ("psum", [128, 8 * BANK], "float32"), "f0": ("sbuf", [32, 128], "bfloat16"),
+           "zb": ("sbuf", [32, 128], "bfloat16"), "n4": ("sbuf", [128, 32], "bfloat16"),
+           "lt": ("sbuf", [32, 32], "float32"), "fr": ("sbuf", [32, 192], "bfloat16"),
+           "off": ("sbuf", [128, 24], "uint16"), "ooff": ("sbuf", [128, 4], "uint16"), "poff": ("sbuf", [128, 4], "uint16"),
+           "loff": ("sbuf", [128, 32], "uint16"), "zoff": ("sbuf", [128, 8], "uint16"), "toff": ("sbuf", [128, 8], "uint16"),
+           "aboff": ("sbuf", [128, 8], "uint16"), "soff": ("sbuf", [128, 2], "uint16")}
+for _n, _w in (("xt", 512), ("zt", 512), ("rtt", 512), ("wt", 2048), ("ut", 512), ("ur", 512), ("vt", 512),
+               ("ht", 4 * END), ("cb", 128), ("tmp", 256), ("tms", 256), ("zw", TW), ("r8", 8), ("tr", 32), ("rk", TW),
+               ("nm", FW), ("ct", FW), ("ov", FW), ("role", FW), ("ma", FW), ("mb", FW), ("dd", FW), ("win", FW), ("cw", FW),
+               ("hf", FW)):
+    SCRATCH[_n] = ("sbuf", [128, _w], "bfloat16")
+for _n, _w in (("xq", 2 * LEAST), ("rq", 128), ("rp", 128), ("wq", 512), ("uq", 128), ("vq", 128), ("xd", 384),
+               ("xf", LEAST + 2), ("xr", END), ("hq0", 192), ("hq1", 128), ("hq2", 128), ("hr", END), ("zq", 128)):
+    SCRATCH[_n] = ("sbuf", [128, _w], "float8_e4m3fn_x4")
+    SCRATCH[_n + "s"] = ("sbuf", [128, _w], "uint8")
+for _n, _w in (("ci", 224), ("cc", 224), ("c2", 4), ("bc", 1), ("sc", 1), ("bx", FW), ("pm", FW), ("zero", TW), ("d0", 64),
+               ("thr", 8), ("c8", 8), ("seg", 128), ("bs", 64), ("cp", 64), ("sg", 64), ("lc", 4), ("of", 32),
+               ("p1", FW), ("p2", FW), ("va", TW), ("vb", TW), ("ta", TW), ("tb", TW), ("lab", 256), ("tab", 2 * END),
+               ("qw", END), ("yw", END), ("ga", FW), ("gb", FW), ("xp", FW), ("val", TW), ("tv", TW), ("s8", 128),
+               ("wnr", 128), ("ysb", 128)):
+    SCRATCH[_n] = ("sbuf", [128, _w], "float32")
+DMAS = ["dx", "drt", "dw0", "dw1", "du", "dv", "doc", "dos0", "dos1", "dos2", "dos3", "dy", "dwn"]
+SEMAPHORES = ["cv", "cs", "ct", "cg", "ls", "xf", "xl", "xa0", "xa1", "xa2", "ha0", "ha1", "ha2"] + DMAS
+
+
+def _runner(g, T):
+    queues = {"v": g.vector, "s": g.scalar, "t": g.tensor, "g": g, "y": g.sync}
+    own = {"v": "cv", "s": "cs", "t": "ct", "g": "cg"}
+    total, known, snap, recs = {}, {q: {} for q in queues}, {}, {}
+
+    def region(view):
+        b, p0, p1, c0, c1, st = view
+        if SCRATCH[b][0] == "psum":
+            return (0, 128, c0 // BANK * BANK, -(-c1 // BANK) * BANK, 1)
+        return (p0, p1, c0, c1, st)
+
+    def meet(a, b):
+        if a[0] >= b[1] or b[0] >= a[1] or a[2] >= b[3] or b[2] >= a[3]:
+            return False
+        return not (a[4] > 1 and a[4] == b[4] and (a[2] - b[2]) % a[4])
+
+    def wait_for(q, need):
+        need = [(s, v) for s, v in need.items() if known[q].get(s, 0) < v]
+        for i, (s, v) in enumerate(need):
+            if any(snap.get(o, {}).get(s, 0) >= v for j, o in enumerate(need) if j != i):
+                continue
+            queues[q].wait_ge(T.sem[s], v)
+        for s, v in need:
+            known[q][s] = max(known[q].get(s, 0), v)
+            for s2, v2 in snap.get((s, v), {}).items():
+                known[q][s2] = max(known[q].get(s2, 0), v2)
+
+    def wants(q, outs, ins):
+        need = {}
+        for wr, views in ((True, outs), (False, ins)):
+            for view in views:
+                r = region(view)
+                ps = SCRATCH[view[0]][0] == "psum"
+                for w, r2, tok, q2 in recs.get(view[0], []):
+                    if not (wr or w or (ps and q2 != q)) or not meet(r, r2):
+                        continue
+                    need[tok[0]] = max(need.get(tok[0], 0), tok[1])
+        return need
+
+    def note(q, outs, ins, tok):
+        for wr, views in ((True, outs), (False, ins)):
+            for view in views:
+                recs.setdefault(view[0], []).append((wr, region(view), tok, q))
+
+    def op(q, call, outs, ins, dma=None):
+        wait_for(q, wants(q, outs, ins))
+        sem, n = (dma, 16) if dma else (own[q], 1)
+        call(queues[q]).then_inc(T.sem[sem], n)
+        total[sem] = total.get(sem, 0) + n
+        tok = (sem, total[sem])
+        snap[tok] = dict(known[q])
+        note(q, outs, ins, tok)
+
+    def arrive(sem, n, outs):
+        total[sem] = total.get(sem, 0) + n
+        note("far", outs, [], (sem, total[sem]))
+
+    def send(call, ins, ls):
+        wait_for("g", wants("g", [], ins))
+        call(g)
+        total["ls"] = total.get("ls", 0) + ls
+
+    def finish():
+        wait_for("g", dict(total))
+
+    return op, arrive, send, finish
+
+
+def rank_program(g, core, T, topo):
+    rank = T.rank_of(core)
+    if rank is None:
+        return
+    op, arrive, send, finish = _runner(g, T)
+    N = len(T.cores)
+
+    def who(i):
+        return rank ^ i
+
+    batch = []
+    for p0, n in ((0, 4), (4, 2), (6, 2)):
+        c0, c1 = Z0 + CAPP * p0, Z0 + CAPP * (p0 + n)
+        batch.append((list(range(p0, p0 + n)), c0, c1, min(c0, c1 - LEAST), c1))
+    chip = [topo.chip(c) for c in T.cores]
+    away = topo.engines(core, next(c for c in T.cores if topo.chip(c) != topo.chip(core)))
+    peer = next(c for c in T.cores if topo.chip(c) == topo.chip(core) and c != core)
+    every = topo.engines(core, peer)
+    near = [e for e in every if e not in away][:len(away) // 2]
+
+    def bits(es):
+        return sum(1 << e for e in es)
+
+    def V(b, c0=0, c1=None, p0=0, p1=None, st=1):
+        sh = SCRATCH[b][1]
+        return (b, p0, sh[0] if p1 is None else p1, c0, sh[1] if c1 is None else c1, st)
+
+    def ap(v):
+        b, p0, p1, c0, c1, st = v
+        return T[b][p0:p1, c0:c1] if st == 1 else T[b][p0:p1, c0:c1:st]
+
+    def by(v):
+        return ap(v).bitcast(dt.uint8)
+
+    def memset(v, x):
+        op("v", lambda q: q.memset(ap(v), x), [v], [])
+
+    def act(out, in_, f, lst=None, acc=None, **k):
+        src = ap(in_) if lst is None else ap(in_).indirect(ap(lst))
+        cols = [x for x in k.values() if isinstance(x, tuple)]
+        kk = {n: ap(x) if isinstance(x, tuple) else x for n, x in k.items()}
+        if acc is not None:
+            kk["accum_out"] = ap(acc)
+        op("s", lambda q: q.activation(ap(out), src, f, **kk), [out] + ([acc] if acc else []),
+           [in_] + cols + ([lst] if lst else []))
+
+    def fill(v, x):
+        n = len(range(v[3], v[4], v[5]))
+        act(v, V("zero", 0, n, v[1], v[2]), ACT.Identity, bias=x)
+
+    def copy(out, in_, q="v", lst=None):
+        if q == "v":
+            src = ap(in_) if lst is None else ap(in_).indirect(ap(lst))
+            op("v", lambda e: e.tensor_copy(ap(out), src), [out], [in_] + ([lst] if lst else []))
+        else:
+            act(out, in_, ACT.Copy, lst)
+
+    def tt(out, a, b, o):
+        op("v", lambda q: q.tensor_tensor(ap(out), ap(a), ap(b), o), [out], [a, b])
+
+    def ts(out, a, s1, o1, s2=None, o2=None):
+        ins = [a] + [s for s in (s1, s2) if isinstance(s, tuple)]
+        x1, x2 = (ap(s) if isinstance(s, tuple) else s for s in (s1, s2))
+        if o2 is None:
+            op("v", lambda q: q.tensor_scalar(ap(out), ap(a), x1, None, o1), [out], ins)
+        else:
+            op("v", lambda q: q.tensor_scalar(ap(out), ap(a), x1, x2, o1, o2), [out], ins)
+
+    def total(out, in_):
+        op("v", lambda e: e.tensor_reduce(ap(out), ap(in_), AxisListType.X, OP.add), [out], [in_])
+
+    def runs(out, mask, in_):
+        op("v", lambda q: q.tensor_tensor_scan(ap(out), ap(mask), ap(in_), 0.0, OP.mult, OP.add), [out], [mask, in_])
+
+    def scan(out, a, b, init):
+        ini = ap(init) if isinstance(init, tuple) else init
+        op("v", lambda q: q.tensor_tensor_scan(ap(out), ap(a), ap(b), ini, OP.add, OP.add), [out],
+           [a, b] + ([init] if isinstance(init, tuple) else []))
+
+    def turn(out, in_):
+        op("v", lambda q: q.transpose(ap(out), ap(in_)), [out], [in_])
+
+    def quant(c, t, a=0, b=None, d=0):
+        n = SCRATCH[t][1][1] // 4 if b is None else b - a
+        o, s, i = V(c, d, d + n), V(c + "s", d, d + n), V(t, 4 * a, 4 * (a + n))
+        op("v", lambda q: q.quantize_mx(ap(o), ap(s), ap(i)), [o, s], [i])
+
+    def mm(bank, l, la, r, ra, rb):
+        out, lc, ls, rc, rs = V("ps", BANK * bank, BANK * bank + rb - ra), V(l, la, la + 128), V(l + "s", la, la + 128), V(r, ra, rb), V(r + "s", ra, rb)
+        op("t", lambda q: q.matmul_mx(ap(out), ap(lc), ap(ls), ap(rc), ap(rs), True, True), [out], [lc, ls, rc, rs])
+
+    def pick(o, w, lst):
+        op("v", lambda q: q.tensor_copy(ap(o).bitcast(dt.uint32), ap(w).bitcast(dt.uint32).indirect(ap(lst))), [o], [w, lst])
+
+    def picks(dst, d, lst, src="xq"):
+        n = 16 * (lst[4] - lst[3])
+        pick(V(dst, d, d + n), V(src), lst)
+        act(V(dst + "s", d, d + n), V(src + "s"), ACT.Copy, lst)
+
+    def dma(q, sem, dst, src, outs, ins):
+        op(q, lambda e: e.dma_start(dst, src), outs, ins, dma=sem)
+
+    def transfer(to, eng, sem, src, dst):
+        rid, pid, _s = topo.addr(to)
+        return RemoteDMATransfer(dst_ids=[DstId(rid=rid, pnc=pid)], dma_engine_mask=bits(eng), remote_sem=T.sem[sem], src=src, dst=dst)
+
+    def to_peer(eng, sem, s, d, f):
+        send(lambda q: q.remote_dma_fused([transfer(peer, eng, sem, f(s), f(d))], local_sem=T.sem["ls"]), [s], len(eng))
+
+    def parts(places):
+        to = [i for i in places if i > 0]
+        far = [i for i in to if chip[who(i)] != topo.chip(core)]
+        return to, far, len(away) // max(len(far), 1)
+
+    def ship(places, src, s0, dst, sem):
+        to, far, k = parts(places)
+        for x, f in (("", by), ("s", ap)):
+            trs, ins, ls = [], [], 0
+            for i in to:
+                eng = near if i not in far else away[k * far.index(i):k * far.index(i) + k]
+                a, d0 = s0(i), Z0 + CAPP * i
+                s, d = V(src + x, a, a + CAPP), V(dst + x, d0, d0 + CAPP)
+                trs.append(transfer(T.cores[who(i)], eng, sem, f(s), f(d)))
+                ins.append(s)
+                ls += len(eng)
+            send(lambda q: q.remote_dma_fused(trs, local_sem=T.sem["ls"]), ins, ls)
+
+    def land(places, dst, sem):
+        to, far, k = parts(places)
+        n = 2 * (len(far) * k + len(near) * (len(to) - len(far)))
+        arrive(sem, n, [V(dst + x, Z0 + CAPP * i, Z0 + CAPP * i + CAPP) for i in to for x in ("", "s")])
+
+    dma("s", "drt", ap(V("rtt", 0, 4 * N)), T.rt[:, 0:4 * N], [V("rtt", 0, 4 * N)], [])
+    dma("y", "dx", ap(V("xt")), T.x[:, :], [V("xt")], [])
+    dma("y", "dv", ap(V("vt")), T.v[:, :], [V("vt")], [])
+    dma("y", "dw0", ap(V("wt", 0, 1024)), T.w[:, 0:1024], [V("wt", 0, 1024)], [])
+    dma("y", "dw1", ap(V("wt", 1024, 2048)), T.w[:, 1024:2048], [V("wt", 1024, 2048)], [])
+    dma("y", "du", ap(V("ut")), T.u[:, :], [V("ut")], [])
+
+    def iota(v, pattern, b, cm=0):
+        op("g", lambda q: q.iota(ap(v), pattern, b, cm, allow_small_or_imprecise_dtypes=True), [v], [])
+
+    def steps(w):
+        return [[-w * b if rank & b else w * b, 2] for b in (4, 2, 1)], w * rank
+
+    iota(V("ci", 0, 32), [[0, 4], [1, 8]], 0)
+    iota(V("ci", 32, 64), [[0, 2], [1, 2], [0, 8]], 0)
+    iota(V("c2"), [[2, 4]], 0)
+    iota(V("ci", 64, 88), [[0, 8], [-16, 3]], 0, -4)
+    iota(V("ci", 88, 96), [[0, 8]], 0)
+    iota(V("ci", 96, 128), [[0, 8], [1, 4]], 0)
+    iota(V("thr"), [[-1, 8]], 7)
+    iota(V("c8"), [[-1, 8]], 8)
+    iota(V("ci", 160, 192), [[0, 2], [1, 2], [0, 8]], -1)
+    iota(V("ci", 192, 224), [[16, 2], [16, 16]], -1)
+    ecol, hcol, mcol, pcol, gcol, lcol = (V("cc", c, c + 1) for c in (0, 32, 96, 128, 160, 192))
+    memset(V("zero"), 0.0)
+    memset(V("rtt", 4 * N, 512), 0.0)
+    memset(V("d0"), 1.0)
+    memset(V("d0", 9, 64, st=9), -1.0)
+    memset(V("d0", 0, 64, st=8), 0.0)
+    turn(V("cc", 0, 64), V("ci", 0, 64))
+    ts(V("aboff", 0, 4), V("c2"), hcol, OP.add, ecol, OP.min)
+    ts(V("aboff", 4, 8), V("c2"), hcol, OP.add, ecol, OP.max)
+    for c in range(0, 512, TW):
+        fill(V("zt", c, min(c + TW, 512)), 0.0)
+    fill(V("n4", 24, 32), 0.0)
+    fill(V("zb"), 0.0)
+
+    quant("rq", "rtt")
+    pick(V("rp"), V("rq"), V("aboff"))
+    act(V("rps"), V("rqs"), ACT.Copy, V("aboff"))
+    quant("xq", "xt", 0, LEAST)
+    mm(0, "xq", 0, "rp", 0, 128)
+    quant("xq", "zt", 0, LEAST, LEAST)
+    to_peer(every, "xf", V("xq", 0, LEAST + 2), V("xf"), by)
+    to_peer(every, "xf", V("xqs", 0, LEAST + 2), V("xfs"), ap)
+    copy(V("bs"), V("ps", 64, 128))
+    turn(V("cc", 64, 128), V("ci", 64, 128))
+    tt(V("cp"), V("ps", 0, 64), V("bs"), OP.is_ge)
+    runs(V("sg"), V("d0"), V("cp"))
+    ts(V("bc"), mcol, 1.5, OP.is_ge, 64.0, OP.mult)
+    rank8 = V("sg", 7, 64, st=8)
+    for k in range(3):
+        tt(V("n4", k, 24, st=3), rank8, V("thr"), OP.is_ge)
+    tt(V("r8"), V("c8"), rank8, OP.subtract)
+    for c0 in (0, 160):
+        fill(V("fr", c0, c0 + 32), 8.0)
+    fill(V("zw"), 0.0)
+    for c in range(0, 4 * Z0, TW):
+        fill(V("ht", c, c + TW), 0.0)
+    for b in ("val", "va", "vb"):
+        fill(V(b, FW, TW), 0.0)
+    fill(V("seg"), 1.0)
+    fill(V("qw", 0, Z0), -BIG)
+    fill(V("yw", 0, Z0), 0.0)
+    fill(V("seg", 0, 128, st=16), 0.0)
+    for a in range(4):
+        turn(V("f0", 32 * a, 32 * a + 32), V("n4", 0, 32, 32 * a, 32 * a + 32))
+    ts(V("sc"), V("bc"), -1.0 / 128, OP.mult, 1.0, OP.add)
+    for a in range(4):
+        scan(V("cb", 0, 128, 32 * a, 32 * a + 32), V("f0"), V("zb"), V("cc", 64 + a, 65 + a, 0, 32))
+    for j in range(4):
+        copy(V("tr", 8 * j, 8 * j + 8), V("r8"), "s")
+    for m in (2, 3):
+        act(V("tms", 128 * m - 256, 128 * m - 128), V("cb"), ACT.Sign, acc=V("lc", m, m + 1), bias=m + 0.5, scale=-1.0)
+    turn(V("cc", 160, 224), V("ci", 160, 224))
+    for m in (0, 1):
+        ts(V("tmp", 128 * m, 128 * m + 128), V("cb"), float(m), OP.is_le)
+    for m in (0, 1):
+        total(V("lc", m, m + 1), V("tmp", 128 * m, 128 * m + 128))
+    ts(V("soff", 0, 1), lcol, 0.0, OP.max, 255.0, OP.min)
+    for a in range(4):
+        for d in (0, 16):
+            copy(V("lt", d + 4 * a, d + 4 * a + 4), V("lc", 0, 4, 32 * a, 32 * a + 32), "s" if d else "v")
+    ts(V("soff", 1, 2), lcol, 128.0, OP.add, 255.0, OP.min)
+    for a in range(4):
+        turn(V("of", 0, 32, 32 * a, 32 * a + 32), V("lt"))
+    ts(V("off"), V("of", 0, 24), V("sc"), OP.mult, V("bc"), OP.add)
+
+    def pair(i, sem):
+        e = who(i) // 2 * 2
+        picks("xd", CAPP * e, V("off", 3 * e, 3 * e + 6))
+        ship([i, i + 1], "xd", lambda j: CAPP * who(j), "xr", sem)
+
+    pair(2, "xa0")
+    to_peer(near, "xl", V("off", 3 * who(1), 3 * who(1) + 3), V("poff", 0, 3), ap)
+    pair(4, "xa1")
+    pair(6, "xa2")
+    if rank % 2:
+        copy(V("ooff", 0, 3), V("off", 3 * rank, 3 * rank + 3))
+    picks("xr", Z0, V("ooff", 0, 3) if rank % 2 else V("off", 3 * rank, 3 * rank + 3))
+    up, at = steps(CAPP)
+    for k in range(4):
+        iota(V("ci", 128 + 8 * k, 136 + 8 * k), up, Z0 - 1 + at)
+    iota(V("bx", 0, 128), [[0, 4], [1, 2], [0, 16]], 0)
+    iota(V("bx", 128, FW), [[0, 16]], 0)
+
+    for a in range(4):
+        turn(V("fr", 32 + 32 * a, 64 + 32 * a), V("tr", 0, 32, 32 * a, 32 * a + 32))
+    quant("wq", "wt")
+    for a in range(4):
+        copy(V("rk", 0, FW, 32 * a, 32 * a + 32), V("fr", 32, 32 + FW), "v" if a > 1 else "s")
+    for a in range(4):
+        copy(V("rk", 0, FW, 32 * a, 32 * a + 16), V("fr", 16, 16 + FW, 0, 16), "v" if a > 1 else "s")
+    arrive("xf", 2 * len(every), [V("xf"), V("xfs")])
+    arrive("xl", len(near), [V("poff", 0, 3)])
+    picks("xr", Z0 + CAPP, V("poff", 0, 3), "xf")
+    for t in range(4):
+        fill(V("ur", t, 512, st=4), V("ut", t, t + 1))
+    ts(V("nm"), V("rk", 0, FW), 1.0, OP.is_le)
+    scan(V("ct"), V("nm"), V("zw", 0, FW), 0.0)
+    quant("uq", "ur")
+    act(V("ov"), V("ct"), ACT.Relu, scale=2.0, bias=-2.0 * CAPP)
+
+    for h, (places, c0, c1, w0, w1) in enumerate(batch):
+        land([i for i in places if i > 1], "xr", "xa%d" % h)
+        banks = [4 * (h % 2) + i for i in range(4)]
+        for i in (0, 2, 1, 3):
+            mm(banks[i], "wq", 128 * i, "xr", w0, w1)
+        for i in range(4):
+            r, o = V("ps", BANK * banks[i] + c0 - w0, BANK * banks[i] + c1 - w0), V("ht", 4 * c0 + i, 4 * c1, st=4)
+            if i < 2:
+                ts(o, r, 0.0, OP.max, 0.0625, OP.mult)
+            else:
+                act(o, r, ACT.Relu, scale=0.0625)
+        quant("hq%d" % h, "ht", w0, w1)
+        ship(places, "hq%d" % h, lambda i: Z0 + CAPP * i - w0, "hr", "ha%d" % h)
+        if h == 0:
+            turn(V("cc", 128, 160), V("ci", 128, 160))
+        elif h == 1:
+            act(V("pm"), V("bx"), ACT.Abs, bias=gcol)
+            act(V("p1"), V("ct"), ACT.Identity, bias=pcol)
+
+    up, at = steps(1)
+    iota(V("tab", END - Z0, END + Z0 - 1), [[0, 2 * Z0 - 1]], -100)
+    for b in (0, 1):
+        c = END - 1 + Z0 + 4 * CAPP * b
+        iota(V("tab", c, c + 4 * CAPP), up[1:] + [[0, CAPP]], at + b * up[0][0])
+        c = 4 * CAPP * b
+        iota(V("tab", c, c + 4 * CAPP), up[1:] + [[0, CAPP]], -1 - who(7) + b * up[0][0])
+
+    tt(V("role"), V("rk", 0, FW), V("ov"), OP.add)
+    tt(V("p2"), V("p1"), V("pm"), OP.mult)
+    act(V("ma"), V("role"), ACT.Relu, scale=-1.0, bias=1.0)
+    ts(V("mb"), V("role"), 1.0, OP.is_equal)
+    quant("hr", "ht", 0, LEAST)
+    tt(V("vb", 0, FW), V("mb"), V("p2"), OP.mult)
+    tt(V("va", 0, FW), V("ma"), V("p2"), OP.mult)
+    turn(V("tb"), V("vb"))
+    turn(V("ta"), V("va"))
+    runs(V("lab", 128, 256), V("seg"), V("tb", 8, 136))
+    runs(V("lab", 0, 128), V("seg"), V("ta", 8, 136))
+    quant("vq", "vt")
+    copy(V("loff"), V("lab"), "v", V("soff"))
+
+    last = len(batch) - 1
+    cuts = ((0, CUT), (CUT, FW))
+    for h, (places, c0, c1, w0, w1) in enumerate(batch):
+        land(places, "hr", "ha%d" % h)
+        mm(h, "uq", 0, "hr", w0, w1)
+        copy(V("qw", c0, c1), V("ps", BANK * h + c0 - w0, BANK * h + c1 - w0), "v" if h == last else "s")
+    for a, b in cuts:
+        copy(V("ga", a, b), V("qw"), "v", V("loff", a // 16, b // 16))
+        copy(V("gb", a, b), V("qw"), "s", V("loff", 16 + a // 16, 16 + b // 16))
+    for h, (places, c0, c1, w0, w1) in enumerate(batch):
+        mm(4 + h, "vq", 0, "hr", w0, w1)
+        copy(V("yw", c0, c1), V("ps", BANK * (4 + h) + c0 - w0, BANK * (4 + h) + c1 - w0), "s")
+    for a, b in cuts:
+        tt(V("dd", a, b), V("gb", a, b), V("ga", a, b), OP.is_gt)
+    for a, b in cuts:
+        tt(V("win", a, b), V("dd", a, b), V("role", a, b), OP.is_equal)
+    for a, b in cuts:
+        scan(V("cw", a, b), V("win", a, b), V("zw", a, b), V("cw", a - 1, a) if a else 0.0)
+        act(V("hf", a, b), V("cw", a, b), ACT.Sign, bias=CAPR + 0.5, scale=-1.0)
+        tt(V("xp", a, b), V("win", a, b), V("p2", a, b), OP.mult)
+    for a, b in cuts:
+        tt(V("val", a, b), V("xp", a, b), V("hf", a, b), OP.mult)
+    turn(V("tv", 0, CUT), V("val", 0, CUT))
+    turn(V("tv", CUT, TW), V("val", CUT, TW))
+    for a, b in ((0, CUT - 16), (CUT - 16, 128)):
+        runs(V("s8", a, b), V("seg", a, b), V("tv", 8 + a, 8 + b))
+    s = V("s8", 15, 128, st=16)
+    copy(V("zoff"), s)
+    ts(V("toff"), s, float(END - 1), OP.add)
+    pick(V("zq"), V("hr"), V("zoff"))
+    dma("y", "doc", T.oc[:, :], by(V("zq")), [], [V("zq")])
+    act(V("ysb"), V("yw"), ACT.Copy, V("zoff"))
+    dma("y", "dy", T.y[:, :], ap(V("ysb")), [], [V("ysb")])
+    copy(V("zqs"), V("hrs"), "v", V("zoff"))
+    act(V("wnr"), V("tab", 0, 2 * END - 1), ACT.Copy, V("toff"))
+    for k in range(3):
+        dma("y", "dos%d" % k, T.osc[4 * k:4 * k + 4, :], ap(V("zqs", 0, 128, 32 * k, 32 * k + 4)), [], [V("zqs")])
+    dma("s", "dwn", T.wn[:, :], ap(V("wnr", 0, 128, 0, 1)), [], [V("wnr", 0, 128, 0, 1)])
+    dma("s", "dos3", T.osc[12:16, :], ap(V("zqs", 0, 128, 96, 100)), [], [V("zqs")])
+    finish()

@@ -11,27 +11,27 @@ CUT = 96
 TW = 160
 BIG = 9e29
 BANK = 512
+UNIT = 1024.0
+BATCH = ((0, 3), (3, 3), (6, 2))
 
 SCRATCH = {"ps": ("psum", [128, 8 * BANK], "float32"), "f0": ("sbuf", [32, 128], "bfloat16"),
-           "zb": ("sbuf", [32, 128], "bfloat16"), "n4": ("sbuf", [128, 32], "bfloat16"),
-           "lt": ("sbuf", [32, 32], "float32"), "fr": ("sbuf", [32, 192], "bfloat16"),
-           "off": ("sbuf", [128, 24], "uint16"), "ooff": ("sbuf", [128, 4], "uint16"), "poff": ("sbuf", [128, 4], "uint16"),
-           "loff": ("sbuf", [128, 32], "uint16"), "zoff": ("sbuf", [128, 8], "uint16"), "toff": ("sbuf", [128, 8], "uint16"),
-           "aboff": ("sbuf", [128, 8], "uint16"), "soff": ("sbuf", [128, 2], "uint16")}
-for _n, _w in (("xt", 512), ("zt", 512), ("rtt", 512), ("wt", 2048), ("ut", 512), ("ur", 512), ("vt", 512),
-               ("ht", 4 * END), ("cb", 128), ("tmp", 256), ("tms", 256), ("zw", TW), ("r8", 8), ("tr", 32), ("rk", TW),
-               ("nm", FW), ("ct", FW), ("ov", FW), ("role", FW), ("ma", FW), ("mb", FW), ("dd", FW), ("win", FW), ("cw", FW),
-               ("hf", FW)):
+           "zb": ("sbuf", [32, 128], "bfloat16"), "lt": ("sbuf", [32, 32], "float32"), "fr": ("sbuf", [32, 192], "bfloat16")}
+for _n, _w in (("off", 32), ("poff", 4), ("loff", 32), ("zoff", 16), ("toff", 16), ("aboff", 8), ("soff", 6), ("noff", 2), ("roff", 2)):
+    SCRATCH[_n] = ("sbuf", [128, _w], "uint16")
+for _n, _w in (("xt", 512), ("rtt", 544), ("wt", 2048), ("ut", 8), ("ur", 512), ("vt", 512), ("n4", 32),
+               ("ht", 4 * END), ("cb", 128), ("tmp", 256), ("tms", 256), ("zw", TW), ("tr", 32), ("bi", 64), ("bt", 64), ("se", 32),
+               ("rk", TW), ("nm", FW), ("ct", FW), ("ov", FW), ("role", FW), ("ma", FW), ("dd", FW), ("lim", 3 * FW), ("seg2", TW),
+               ("cin", 1), ("d0", 64), ("cp", 64), ("sg", 64), ("seg", TW)):
     SCRATCH[_n] = ("sbuf", [128, _w], "bfloat16")
-for _n, _w in (("xq", 2 * LEAST), ("rq", 128), ("rp", 128), ("wq", 512), ("uq", 128), ("vq", 128), ("xd", 384),
-               ("xf", LEAST + 2), ("xr", END), ("hq0", 192), ("hq1", 128), ("hq2", 128), ("hr", END), ("zq", 128)):
+for _n, _w in (("tri", 3 * FW), ("va", TW), ("ta", TW), ("val", 3 * TW), ("tv", TW)):
+    SCRATCH[_n] = ("sbuf", [128, _w], "float16")
+for _n, _w in (("xq", 2 * LEAST), ("rq", 128), ("rp", 128), ("wq", 512), ("uq", 128), ("vq", 128), ("xd", 512),
+               ("xf", LEAST + 2), ("xr", END), ("hq0", 144), ("hq1", 144), ("hq2", 144), ("hr", END), ("zq", 128)):
     SCRATCH[_n] = ("sbuf", [128, _w], "float8_e4m3fn_x4")
     SCRATCH[_n + "s"] = ("sbuf", [128, _w], "uint8")
-for _n, _w in (("ci", 224), ("cc", 224), ("c2", 4), ("bc", 1), ("sc", 1), ("bx", FW), ("pm", FW), ("zero", TW), ("d0", 64),
-               ("thr", 8), ("c8", 8), ("seg", 128), ("bs", 64), ("cp", 64), ("sg", 64), ("lc", 4), ("of", 32),
-               ("p1", FW), ("p2", FW), ("va", TW), ("vb", TW), ("ta", TW), ("tb", TW), ("lab", 256), ("tab", 2 * END),
-               ("qw", END), ("yw", END), ("ga", FW), ("gb", FW), ("xp", FW), ("val", TW), ("tv", TW), ("s8", 128),
-               ("wnr", 128), ("ysb", 128)):
+for _n, _w in (("ci", 288), ("cc", 288), ("c2", 4), ("bc", 1), ("sc", 1), ("c8", 32), ("s8", TW),
+               ("thr", 32), ("bs", 64), ("lc", 4), ("of", 32), ("lab", TW), ("tab", 2 * END),
+               ("qw", END), ("yw", END), ("ga", FW), ("gb", FW), ("wnr", 16), ("ysb", 128)):
     SCRATCH[_n] = ("sbuf", [128, _w], "float32")
 DMAS = ["dx", "drt", "dw0", "dw1", "du", "dv", "doc", "dos0", "dos1", "dos2", "dos3", "dy", "dwn"]
 SEMAPHORES = ["cv", "cs", "ct", "cg", "ls", "xf", "xl", "xa0", "xa1", "xa2", "ha0", "ha1", "ha2"] + DMAS
@@ -112,18 +112,24 @@ def rank_program(g, core, T, topo):
     op, arrive, send, finish = _runner(g, T)
     N = len(T.cores)
 
-    def who(i):
-        return rank ^ i
+    def kind(i):
+        c = T.cores[rank ^ i]
+        return (topo.chip(c) == topo.chip(core), topo.die(c) == topo.die(core))
 
-    batch = []
-    for p0, n in ((0, 4), (4, 2), (6, 2)):
-        c0, c1 = Z0 + CAPP * p0, Z0 + CAPP * (p0 + n)
-        batch.append((list(range(p0, p0 + n)), c0, c1, min(c0, c1 - LEAST), c1))
-    chip = [topo.chip(c) for c in T.cores]
-    away = topo.engines(core, next(c for c in T.cores if topo.chip(c) != topo.chip(core)))
-    peer = next(c for c in T.cores if topo.chip(c) == topo.chip(core) and c != core)
-    every = topo.engines(core, peer)
-    near = [e for e in every if e not in away][:len(away) // 2]
+    peer = [i for i in range(1, N) if kind(i)[0]]
+    same = [i for i in range(1, N) if kind(i) == (False, True)]
+    other = [i for i in range(1, N) if kind(i) == (False, False)]
+    order = [0, same[0], other[0], peer[0], other[1], same[1], other[2], same[2]]
+
+    def who(p):
+        return rank ^ order[p]
+
+    place = [order.index(e ^ rank) for e in range(N)]
+    batch = [(list(range(p0, p0 + n)), Z0 + CAPP * p0, Z0 + CAPP * (p0 + n)) for p0, n in BATCH]
+    sent = [[p for p in bt[0] if p > 1] for bt in batch]
+    back = [[p for p in bt[0] if p > 0] for bt in batch]
+    away = topo.engines(core, T.cores[who(1)])
+    near = [e for e in topo.engines(core, T.cores[rank ^ peer[0]]) if e not in away][:len(away) // 2]
 
     def bits(es):
         return sum(1 << e for e in es)
@@ -139,6 +145,12 @@ def rank_program(g, core, T, topo):
     def by(v):
         return ap(v).bitcast(dt.uint8)
 
+    def zeros(n, p0=0, p1=128):
+        return V("rtt", 4 * N, 4 * N + n, p0, p1)
+
+    def tri(j, a=0, b=FW):
+        return V("tri", 3 * a + j, 3 * b, st=3)
+
     def memset(v, x):
         op("v", lambda q: q.memset(ap(v), x), [v], [])
 
@@ -152,8 +164,7 @@ def rank_program(g, core, T, topo):
            [in_] + cols + ([lst] if lst else []))
 
     def fill(v, x):
-        n = len(range(v[3], v[4], v[5]))
-        act(v, V("zero", 0, n, v[1], v[2]), ACT.Identity, bias=x)
+        act(v, zeros(len(range(v[3], v[4], v[5])), v[1], v[2]), ACT.Identity, bias=x)
 
     def copy(out, in_, q="v", lst=None):
         if q == "v":
@@ -162,27 +173,29 @@ def rank_program(g, core, T, topo):
         else:
             act(out, in_, ACT.Copy, lst)
 
-    def tt(out, a, b, o):
-        op("v", lambda q: q.tensor_tensor(ap(out), ap(a), ap(b), o), [out], [a, b])
+    def tt(out, a, b, o, lst=None):
+        src = ap(a) if lst is None else ap(a).indirect(ap(lst))
+        op("v", lambda q: q.tensor_tensor(ap(out), src, ap(b), o), [out], [a, b] + ([lst] if lst else []))
 
-    def ts(out, a, s1, o1, s2=None, o2=None):
-        ins = [a] + [s for s in (s1, s2) if isinstance(s, tuple)]
+    def ts(out, a, s1, o1, s2=None, o2=None, lst=None):
+        ins = [a] + [s for s in (s1, s2, lst) if isinstance(s, tuple)]
+        src = ap(a) if lst is None else ap(a).indirect(ap(lst))
         x1, x2 = (ap(s) if isinstance(s, tuple) else s for s in (s1, s2))
         if o2 is None:
-            op("v", lambda q: q.tensor_scalar(ap(out), ap(a), x1, None, o1), [out], ins)
+            op("v", lambda q: q.tensor_scalar(ap(out), src, x1, None, o1), [out], ins)
         else:
-            op("v", lambda q: q.tensor_scalar(ap(out), ap(a), x1, x2, o1, o2), [out], ins)
+            op("v", lambda q: q.tensor_scalar(ap(out), src, x1, x2, o1, o2), [out], ins)
 
     def total(out, in_):
         op("v", lambda e: e.tensor_reduce(ap(out), ap(in_), AxisListType.X, OP.add), [out], [in_])
 
-    def runs(out, mask, in_):
-        op("v", lambda q: q.tensor_tensor_scan(ap(out), ap(mask), ap(in_), 0.0, OP.mult, OP.add), [out], [mask, in_])
-
-    def scan(out, a, b, init):
+    def scan(out, a, b, init=0.0, o0=OP.add, o1=OP.add):
         ini = ap(init) if isinstance(init, tuple) else init
-        op("v", lambda q: q.tensor_tensor_scan(ap(out), ap(a), ap(b), ini, OP.add, OP.add), [out],
+        op("v", lambda q: q.tensor_tensor_scan(ap(out), ap(a), ap(b), ini, o0, o1), [out],
            [a, b] + ([init] if isinstance(init, tuple) else []))
+
+    def runs(out, mask, in_):
+        scan(out, mask, in_, 0.0, OP.mult)
 
     def turn(out, in_):
         op("v", lambda q: q.transpose(ap(out), ap(in_)), [out], [in_])
@@ -207,237 +220,237 @@ def rank_program(g, core, T, topo):
     def dma(q, sem, dst, src, outs, ins):
         op(q, lambda e: e.dma_start(dst, src), outs, ins, dma=sem)
 
-    def transfer(to, eng, sem, src, dst):
-        rid, pid, _s = topo.addr(to)
+    def iota(v, pattern, b, cm=0):
+        op("g", lambda q: q.iota(ap(v), pattern, b, cm, allow_small_or_imprecise_dtypes=True), [v], [])
+
+    def table(b, c0, vals, rep):
+        for i in range(0, len(vals), 4):
+            a = vals[i:i + 4]
+            if a[3] - a[2] == a[1] - a[0]:
+                iota(V(b, c0 + rep * i, c0 + rep * (i + 4)), [[a[2] - a[0], 2], [a[1] - a[0], 2], [0, rep]], a[0])
+            else:
+                for j in (0, 2):
+                    iota(V(b, c0 + rep * (i + j), c0 + rep * (i + j + 2)), [[a[j + 1] - a[j], 2], [0, rep]], a[j])
+
+    def transfer(p, eng, sem, src, dst):
+        rid, pid, _s = topo.addr(T.cores[who(p)])
         return RemoteDMATransfer(dst_ids=[DstId(rid=rid, pnc=pid)], dma_engine_mask=bits(eng), remote_sem=T.sem[sem], src=src, dst=dst)
 
-    def to_peer(eng, sem, s, d, f):
-        send(lambda q: q.remote_dma_fused([transfer(peer, eng, sem, f(s), f(d))], local_sem=T.sem["ls"]), [s], len(eng))
+    def early(sem, s, d, f):
+        send(lambda q: q.remote_dma_fused([transfer(1, away, sem, f(s), f(d))], local_sem=T.sem["ls"]), [s], len(away))
 
-    def parts(places):
-        to = [i for i in places if i > 0]
-        far = [i for i in to if chip[who(i)] != topo.chip(core)]
-        return to, far, len(away) // max(len(far), 1)
+    def shares(places):
+        far = [p for p in places if order[p] != peer[0]]
+        k = len(away) // len(far)
+        return [(p, away[k * far.index(p):k * far.index(p) + k] if p in far else near) for p in places]
 
     def ship(places, src, s0, dst, sem):
-        to, far, k = parts(places)
         for x, f in (("", by), ("s", ap)):
             trs, ins, ls = [], [], 0
-            for i in to:
-                eng = near if i not in far else away[k * far.index(i):k * far.index(i) + k]
-                a, d0 = s0(i), Z0 + CAPP * i
+            for p, eng in shares(places):
+                a, d0 = s0(p), Z0 + CAPP * p
                 s, d = V(src + x, a, a + CAPP), V(dst + x, d0, d0 + CAPP)
-                trs.append(transfer(T.cores[who(i)], eng, sem, f(s), f(d)))
+                trs.append(transfer(p, eng, sem, f(s), f(d)))
                 ins.append(s)
                 ls += len(eng)
             send(lambda q: q.remote_dma_fused(trs, local_sem=T.sem["ls"]), ins, ls)
 
     def land(places, dst, sem):
-        to, far, k = parts(places)
-        n = 2 * (len(far) * k + len(near) * (len(to) - len(far)))
-        arrive(sem, n, [V(dst + x, Z0 + CAPP * i, Z0 + CAPP * i + CAPP) for i in to for x in ("", "s")])
+        arrive(sem, sum(2 * len(eng) for p, eng in shares(places)),
+               [V(dst + x, Z0 + CAPP * p, Z0 + CAPP * p + CAPP) for p in places for x in ("", "s")])
 
     dma("s", "drt", ap(V("rtt", 0, 4 * N)), T.rt[:, 0:4 * N], [V("rtt", 0, 4 * N)], [])
     dma("y", "dx", ap(V("xt")), T.x[:, :], [V("xt")], [])
-    dma("y", "dv", ap(V("vt")), T.v[:, :], [V("vt")], [])
+    dma("y", "du", ap(V("ut", 0, 4)), T.u[:, 0:4], [V("ut", 0, 4)], [])
     dma("y", "dw0", ap(V("wt", 0, 1024)), T.w[:, 0:1024], [V("wt", 0, 1024)], [])
     dma("y", "dw1", ap(V("wt", 1024, 2048)), T.w[:, 1024:2048], [V("wt", 1024, 2048)], [])
-    dma("y", "du", ap(V("ut")), T.u[:, :], [V("ut")], [])
-
-    def iota(v, pattern, b, cm=0):
-        op("g", lambda q: q.iota(ap(v), pattern, b, cm, allow_small_or_imprecise_dtypes=True), [v], [])
-
-    def steps(w):
-        return [[-w * b if rank & b else w * b, 2] for b in (4, 2, 1)], w * rank
+    dma("y", "dv", ap(V("vt")), T.v[:, :], [V("vt")], [])
 
     iota(V("ci", 0, 32), [[0, 4], [1, 8]], 0)
     iota(V("ci", 32, 64), [[0, 2], [1, 2], [0, 8]], 0)
     iota(V("c2"), [[2, 4]], 0)
-    iota(V("ci", 64, 88), [[0, 8], [-16, 3]], 0, -4)
-    iota(V("ci", 88, 96), [[0, 8]], 0)
+    table("thr", 0, [N - 1 - who(p) for p in range(N)], 4)
+    iota(V("bi", 0, 32), [[0, 8], [-16, 4]], 0, -4)
+    iota(V("ci", 64, 96), [[0, 32]], 31, 1)
     iota(V("ci", 96, 128), [[0, 8], [1, 4]], 0)
-    iota(V("thr"), [[-1, 8]], 7)
-    iota(V("c8"), [[-1, 8]], 8)
-    iota(V("ci", 160, 192), [[0, 2], [1, 2], [0, 8]], -1)
-    iota(V("ci", 192, 224), [[16, 2], [16, 16]], -1)
-    ecol, hcol, mcol, pcol, gcol, lcol = (V("cc", c, c + 1) for c in (0, 32, 96, 128, 160, 192))
-    memset(V("zero"), 0.0)
-    memset(V("rtt", 4 * N, 512), 0.0)
+    iota(V("ci", 128, 160), [[0, 2], [16, 16]], 7)
+    iota(V("ci", 160, 192), [[-16, 2], [16, 16]], 23)
+    ecol, hcol, qcol, mcol, gcol, lcol, pcol = (V("cc", c, c + 1) for c in (0, 32, 64, 96, 128, 160, 192))
+    memset(zeros(512), 0.0)
     memset(V("d0"), 1.0)
     memset(V("d0", 9, 64, st=9), -1.0)
     memset(V("d0", 0, 64, st=8), 0.0)
     turn(V("cc", 0, 64), V("ci", 0, 64))
     ts(V("aboff", 0, 4), V("c2"), hcol, OP.add, ecol, OP.min)
     ts(V("aboff", 4, 8), V("c2"), hcol, OP.add, ecol, OP.max)
-    for c in range(0, 512, TW):
-        fill(V("zt", c, min(c + TW, 512)), 0.0)
-    fill(V("n4", 24, 32), 0.0)
     fill(V("zb"), 0.0)
+    copy(V("bi", 32, 64), V("ci", 32, 64), "s")
+    for k in range(4):
+        act(V("ci", 224 + 16 * k, 240 + 16 * k), V("thr", 16 * (k // 2), 16 * (k // 2) + 16), ACT.Identity, scale=-8.0, bias=63.0)
+    quant("xq", "rtt", N, N + LEAST, LEAST)
 
-    quant("rq", "rtt")
+    quant("rq", "rtt", 0, LEAST)
+    ts(V("c8"), V("ci", 0, 32), -1.0, OP.mult, 8.0, OP.add)
     pick(V("rp"), V("rq"), V("aboff"))
     act(V("rps"), V("rqs"), ACT.Copy, V("aboff"))
     quant("xq", "xt", 0, LEAST)
     mm(0, "xq", 0, "rp", 0, 128)
-    quant("xq", "zt", 0, LEAST, LEAST)
-    to_peer(every, "xf", V("xq", 0, LEAST + 2), V("xf"), by)
-    to_peer(every, "xf", V("xqs", 0, LEAST + 2), V("xfs"), ap)
+    early("xf", V("xqs", 0, LEAST + 2), V("xfs"), ap)
+    early("xf", V("xq", 0, LEAST + 2), V("xf"), by)
+    fill(V("ht", 0, 4 * Z0), 0.0)
+    turn(V("cc", 224, 288), V("ci", 224, 288))
+    ts(V("roff"), V("cc", 0, 2), 8.0, OP.mult, 7.0, OP.add)
+    turn(V("cc", 64, 192), V("ci", 64, 192))
     copy(V("bs"), V("ps", 64, 128))
-    turn(V("cc", 64, 128), V("ci", 64, 128))
+    copy(V("noff"), V("cc", 224, 288, st=32))
     tt(V("cp"), V("ps", 0, 64), V("bs"), OP.is_ge)
-    runs(V("sg"), V("d0"), V("cp"))
     ts(V("bc"), mcol, 1.5, OP.is_ge, 64.0, OP.mult)
-    rank8 = V("sg", 7, 64, st=8)
-    for k in range(3):
-        tt(V("n4", k, 24, st=3), rank8, V("thr"), OP.is_ge)
-    tt(V("r8"), V("c8"), rank8, OP.subtract)
+    runs(V("sg"), V("d0"), V("cp"))
+    ts(V("sc"), V("bc"), -1.0 / 128, OP.mult, 1.0, OP.add)
+    tt(V("n4"), V("sg"), V("thr"), OP.is_ge, V("noff"))
+    copy(V("se"), V("sg"), "s", V("roff"))
+    turn(V("bt"), V("bi"))
     for c0 in (0, 160):
         fill(V("fr", c0, c0 + 32), 8.0)
     fill(V("zw"), 0.0)
-    for c in range(0, 4 * Z0, TW):
-        fill(V("ht", c, c + TW), 0.0)
-    for b in ("val", "va", "vb"):
-        fill(V(b, FW, TW), 0.0)
-    fill(V("seg"), 1.0)
-    fill(V("qw", 0, Z0), -BIG)
-    fill(V("yw", 0, Z0), 0.0)
-    fill(V("seg", 0, 128, st=16), 0.0)
     for a in range(4):
         turn(V("f0", 32 * a, 32 * a + 32), V("n4", 0, 32, 32 * a, 32 * a + 32))
-    ts(V("sc"), V("bc"), -1.0 / 128, OP.mult, 1.0, OP.add)
+    fill(V("seg"), 1.0)
+    fill(V("seg", 0, TW, st=8), 0.0)
+    copy(V("va", FW, TW), zeros(TW - FW))
     for a in range(4):
-        scan(V("cb", 0, 128, 32 * a, 32 * a + 32), V("f0"), V("zb"), V("cc", 64 + a, 65 + a, 0, 32))
-    for j in range(4):
-        copy(V("tr", 8 * j, 8 * j + 8), V("r8"), "s")
+        scan(V("cb", 0, 128, 32 * a, 32 * a + 32), V("f0"), V("zb"), V("bt", a, a + 1, 0, 32))
+    copy(V("val", 3 * FW + 2, 3 * TW, st=3), zeros(TW - FW))
     for m in (2, 3):
         act(V("tms", 128 * m - 256, 128 * m - 128), V("cb"), ACT.Sign, acc=V("lc", m, m + 1), bias=m + 0.5, scale=-1.0)
-    turn(V("cc", 160, 224), V("ci", 160, 224))
     for m in (0, 1):
         ts(V("tmp", 128 * m, 128 * m + 128), V("cb"), float(m), OP.is_le)
     for m in (0, 1):
         total(V("lc", m, m + 1), V("tmp", 128 * m, 128 * m + 128))
-    ts(V("soff", 0, 1), lcol, 0.0, OP.max, 255.0, OP.min)
+    ts(V("soff", 0, 1), gcol, TW - 1.0, OP.min)
     for a in range(4):
         for d in (0, 16):
             copy(V("lt", d + 4 * a, d + 4 * a + 4), V("lc", 0, 4, 32 * a, 32 * a + 32), "s" if d else "v")
-    ts(V("soff", 1, 2), lcol, 128.0, OP.add, 255.0, OP.min)
-    for a in range(4):
+    ts(V("soff", 1, 2), gcol, 8.0, OP.add, TW - 1.0, OP.min)
+    for a in range(2):
         turn(V("of", 0, 32, 32 * a, 32 * a + 32), V("lt"))
-    ts(V("off"), V("of", 0, 24), V("sc"), OP.mult, V("bc"), OP.add)
+    ts(V("soff", 2, 3), lcol, TW - 1.0, OP.min)
+    for a in range(2):
+        ts(V("off", 0, 32, 64 * a, 64 * a + 64), V("of", 0, 32, 0, 64), V("sc", 0, 1, 0, 64), OP.mult, V("bc", 0, 1, 0, 64), OP.add)
+    tt(V("tr"), V("c8"), V("se"), OP.subtract)
 
-    def pair(i, sem):
-        e = who(i) // 2 * 2
-        picks("xd", CAPP * e, V("off", 3 * e, 3 * e + 6))
-        ship([i, i + 1], "xd", lambda j: CAPP * who(j), "xr", sem)
+    early("xl", V("off", 4, 7), V("poff", 0, 3), ap)
+    for h, to in enumerate(sent):
+        picks("xd", 64 * to[0], V("off", 4 * to[0], 4 * to[-1] + 3))
+        ship(to, "xd", lambda p: 64 * p, "xr", "xa%d" % h)
+    picks("xr", Z0, V("off", 0, 3))
+    copy(V("soff", 4, 5), qcol)
+    table("ci", 192, [Z0 - 1 + CAPP * place[e] for e in range(N)], 1)
 
-    pair(2, "xa0")
-    to_peer(near, "xl", V("off", 3 * who(1), 3 * who(1) + 3), V("poff", 0, 3), ap)
-    pair(4, "xa1")
-    pair(6, "xa2")
-    if rank % 2:
-        copy(V("ooff", 0, 3), V("off", 3 * rank, 3 * rank + 3))
-    picks("xr", Z0, V("ooff", 0, 3) if rank % 2 else V("off", 3 * rank, 3 * rank + 3))
-    up, at = steps(CAPP)
-    for k in range(4):
-        iota(V("ci", 128 + 8 * k, 136 + 8 * k), up, Z0 - 1 + at)
-    iota(V("bx", 0, 128), [[0, 4], [1, 2], [0, 16]], 0)
-    iota(V("bx", 128, FW), [[0, 16]], 0)
-
+    quant("wq", "wt")
+    arrive("xf", 2 * len(away), [V("xf"), V("xfs")])
+    arrive("xl", len(away), [V("poff", 0, 3)])
+    picks("xr", Z0 + CAPP, V("poff", 0, 3), "xf")
     for a in range(4):
         turn(V("fr", 32 + 32 * a, 64 + 32 * a), V("tr", 0, 32, 32 * a, 32 * a + 32))
-    quant("wq", "wt")
-    for a in range(4):
-        copy(V("rk", 0, FW, 32 * a, 32 * a + 32), V("fr", 32, 32 + FW), "v" if a > 1 else "s")
-    for a in range(4):
-        copy(V("rk", 0, FW, 32 * a, 32 * a + 16), V("fr", 16, 16 + FW, 0, 16), "v" if a > 1 else "s")
-    arrive("xf", 2 * len(every), [V("xf"), V("xfs")])
-    arrive("xl", len(near), [V("poff", 0, 3)])
-    picks("xr", Z0 + CAPP, V("poff", 0, 3), "xf")
-    for t in range(4):
-        fill(V("ur", t, 512, st=4), V("ut", t, t + 1))
-    ts(V("nm"), V("rk", 0, FW), 1.0, OP.is_le)
-    scan(V("ct"), V("nm"), V("zw", 0, FW), 0.0)
-    quant("uq", "ur")
-    act(V("ov"), V("ct"), ACT.Relu, scale=2.0, bias=-2.0 * CAPP)
 
-    for h, (places, c0, c1, w0, w1) in enumerate(batch):
-        land([i for i in places if i > 1], "xr", "xa%d" % h)
+    def ranks():
+        for n, c in ((32, 32), (16, 16)):
+            for a in range(2):
+                copy(V("rk", 0, FW, 32 * a, 32 * a + n), V("fr", c, c + FW, 0, n))
+        copy(V("rk", 0, FW, 64, 128), V("rk", 0, FW, 0, 64))
+        for t in range(4):
+            fill(V("ur", t, 512, st=4), V("ut", t, t + 1))
+
+    def over():
+        copy(V("ci", 200, 208), V("ci", 192, 200), "s")
+        copy(V("ci", 208, 224), V("ci", 192, 208), "s")
+        act(V("ov"), V("ct"), ACT.Relu, scale=2.0, bias=-2.0 * CAPP)
+
+    gaps = {(0, 0): ranks, (0, 1): lambda: ts(V("nm"), V("rk", 0, FW), 1.0, OP.is_le),
+            (0, 2): lambda: scan(V("ct"), V("nm"), V("zw", 0, FW)), (0, 3): over,
+            (1, 0): lambda: quant("hr", "ht", 0, LEAST), (1, 1): lambda: turn(V("cc", 192, 224), V("ci", 192, 224)),
+            (1, 2): lambda: ts(tri(1), V("ct"), pcol, OP.add, 1.0 / UNIT, OP.mult)}
+
+    def gap(h, i):
+        if (h, i) in gaps:
+            gaps[h, i]()
+
+    for h, (places, c0, c1) in enumerate(batch):
+        w0 = min(c0, c1 - LEAST)
+        land(sent[h], "xr", "xa%d" % h)
         banks = [4 * (h % 2) + i for i in range(4)]
         for i in (0, 2, 1, 3):
-            mm(banks[i], "wq", 128 * i, "xr", w0, w1)
-        for i in range(4):
+            mm(banks[i], "wq", 128 * i, "xr", w0, c1)
+        for i in (0, 2, 1, 3):
             r, o = V("ps", BANK * banks[i] + c0 - w0, BANK * banks[i] + c1 - w0), V("ht", 4 * c0 + i, 4 * c1, st=4)
             if i < 2:
+                gap(h, i)
                 ts(o, r, 0.0, OP.max, 0.0625, OP.mult)
             else:
                 act(o, r, ACT.Relu, scale=0.0625)
-        quant("hq%d" % h, "ht", w0, w1)
-        ship(places, "hq%d" % h, lambda i: Z0 + CAPP * i - w0, "hr", "ha%d" % h)
-        if h == 0:
-            turn(V("cc", 128, 160), V("ci", 128, 160))
-        elif h == 1:
-            act(V("pm"), V("bx"), ACT.Abs, bias=gcol)
-            act(V("p1"), V("ct"), ACT.Identity, bias=pcol)
+        gap(h, 2)
+        q0 = min(max(c0, LEAST), c1 - LEAST)
+        quant("hq%d" % h, "ht", q0, c1)
+        ship(back[h], "hq%d" % h, lambda p: Z0 + CAPP * p - q0, "hr", "ha%d" % h)
+        gap(h, 3)
 
-    up, at = steps(1)
     iota(V("tab", END - Z0, END + Z0 - 1), [[0, 2 * Z0 - 1]], -100)
-    for b in (0, 1):
-        c = END - 1 + Z0 + 4 * CAPP * b
-        iota(V("tab", c, c + 4 * CAPP), up[1:] + [[0, CAPP]], at + b * up[0][0])
-        c = 4 * CAPP * b
-        iota(V("tab", c, c + 4 * CAPP), up[1:] + [[0, CAPP]], -1 - who(7) + b * up[0][0])
+    table("tab", END - 1 + Z0, [who(p) for p in range(N)], CAPP)
+    table("tab", 0, [-1 - who(N - 1 - p) for p in range(N)], CAPP)
 
+    half = V("bt", 32, 33)
     tt(V("role"), V("rk", 0, FW), V("ov"), OP.add)
-    tt(V("p2"), V("p1"), V("pm"), OP.mult)
-    act(V("ma"), V("role"), ACT.Relu, scale=-1.0, bias=1.0)
-    ts(V("mb"), V("role"), 1.0, OP.is_equal)
-    quant("hr", "ht", 0, LEAST)
-    tt(V("vb", 0, FW), V("mb"), V("p2"), OP.mult)
-    tt(V("va", 0, FW), V("ma"), V("p2"), OP.mult)
-    turn(V("tb"), V("vb"))
+    quant("uq", "ur")
+    fill(V("qw", 0, Z0), -BIG)
+    fill(V("yw", 0, Z0), 0.0)
+    fill(V("lim"), 0.0)
+    copy(V("seg2"), V("seg"), "s")
+    act(V("cin"), half, ACT.Identity, scale=255.5 - CAPR, bias=CAPR + 0.5)
+    fill(V("lim", 0, 3 * FW, st=3), UNIT)
+    fill(V("seg2", 8, TW, st=16), -2.0)
+    ts(V("ma"), V("role"), half, OP.is_equal)
+    tt(V("va", 0, FW), V("ma"), tri(1), OP.mult)
     turn(V("ta"), V("va"))
-    runs(V("lab", 128, 256), V("seg"), V("tb", 8, 136))
-    runs(V("lab", 0, 128), V("seg"), V("ta", 8, 136))
     quant("vq", "vt")
-    copy(V("loff"), V("lab"), "v", V("soff"))
+    runs(V("lab"), V("seg"), V("ta"))
+    ts(V("loff"), V("lab"), UNIT, OP.mult, lst=V("soff", 0, 2))
 
     last = len(batch) - 1
-    cuts = ((0, CUT), (CUT, FW))
-    for h, (places, c0, c1, w0, w1) in enumerate(batch):
-        land(places, "hr", "ha%d" % h)
-        mm(h, "uq", 0, "hr", w0, w1)
+    cuts, blocks = ((0, CUT), (CUT, FW)), ((0, CUT), (CUT, TW))
+    for h, (places, c0, c1) in enumerate(batch):
+        w0 = min(c0, c1 - LEAST)
+        land(back[h], "hr", "ha%d" % h)
+        mm(h, "uq", 0, "hr", w0, c1)
         copy(V("qw", c0, c1), V("ps", BANK * h + c0 - w0, BANK * h + c1 - w0), "v" if h == last else "s")
     for a, b in cuts:
         copy(V("ga", a, b), V("qw"), "v", V("loff", a // 16, b // 16))
         copy(V("gb", a, b), V("qw"), "s", V("loff", 16 + a // 16, 16 + b // 16))
-    for h, (places, c0, c1, w0, w1) in enumerate(batch):
-        mm(4 + h, "vq", 0, "hr", w0, w1)
+    for h, (places, c0, c1) in enumerate(batch):
+        w0 = min(c0, c1 - LEAST)
+        mm(4 + h, "vq", 0, "hr", w0, c1)
         copy(V("yw", c0, c1), V("ps", BANK * (4 + h) + c0 - w0, BANK * (4 + h) + c1 - w0), "s")
     for a, b in cuts:
         tt(V("dd", a, b), V("gb", a, b), V("ga", a, b), OP.is_gt)
     for a, b in cuts:
-        tt(V("win", a, b), V("dd", a, b), V("role", a, b), OP.is_equal)
+        tt(tri(2, a, b), V("dd", a, b), V("role", a, b), OP.is_equal)
+    scan(tri(0), V("zw", 0, FW), tri(2), V("cin"), OP.add, OP.subtract)
     for a, b in cuts:
-        scan(V("cw", a, b), V("win", a, b), V("zw", a, b), V("cw", a - 1, a) if a else 0.0)
-        act(V("hf", a, b), V("cw", a, b), ACT.Sign, bias=CAPR + 0.5, scale=-1.0)
-        tt(V("xp", a, b), V("win", a, b), V("p2", a, b), OP.mult)
-    for a, b in cuts:
-        tt(V("val", a, b), V("xp", a, b), V("hf", a, b), OP.mult)
-    turn(V("tv", 0, CUT), V("val", 0, CUT))
-    turn(V("tv", CUT, TW), V("val", CUT, TW))
-    for a, b in ((0, CUT - 16), (CUT - 16, 128)):
-        runs(V("s8", a, b), V("seg", a, b), V("tv", 8 + a, 8 + b))
-    s = V("s8", 15, 128, st=16)
-    copy(V("zoff"), s)
-    ts(V("toff"), s, float(END - 1), OP.add)
-    pick(V("zq"), V("hr"), V("zoff"))
+        scan(V("val", 3 * a, 3 * b), V("lim", 3 * a, 3 * b), V("tri", 3 * a, 3 * b), 0.0, OP.max, OP.min)
+    for a, b in blocks:
+        turn(V("tv", a, b), V("val", 3 * a + 2, 3 * b, st=3))
+    for a, b in blocks:
+        runs(V("s8", a, b), V("seg2", a, b), V("tv", a, b))
+    z = V("zoff", 0, 8)
+    ts(V("zoff"), V("s8"), UNIT, OP.mult, lst=V("soff", 2, 3))
+    ts(V("toff"), V("s8"), -UNIT, OP.mult, float(END - 1), OP.add, lst=V("soff", 4, 5))
+    pick(V("zq"), V("hr"), z)
     dma("y", "doc", T.oc[:, :], by(V("zq")), [], [V("zq")])
-    act(V("ysb"), V("yw"), ACT.Copy, V("zoff"))
+    act(V("ysb"), V("yw"), ACT.Copy, z)
     dma("y", "dy", T.y[:, :], ap(V("ysb")), [], [V("ysb")])
-    copy(V("zqs"), V("hrs"), "v", V("zoff"))
-    act(V("wnr"), V("tab", 0, 2 * END - 1), ACT.Copy, V("toff"))
-    for k in range(3):
-        dma("y", "dos%d" % k, T.osc[4 * k:4 * k + 4, :], ap(V("zqs", 0, 128, 32 * k, 32 * k + 4)), [], [V("zqs")])
-    dma("s", "dwn", T.wn[:, :], ap(V("wnr", 0, 128, 0, 1)), [], [V("wnr", 0, 128, 0, 1)])
-    dma("s", "dos3", T.osc[12:16, :], ap(V("zqs", 0, 128, 96, 100)), [], [V("zqs")])
+    copy(V("zqs"), V("hrs"), "v", z)
+    act(V("wnr"), V("tab", 0, 2 * END - 1), ACT.Copy, V("toff", 0, 1))
+    dma("s", "dwn", T.wn[:, :], T.wnr[0:128:16, 0:16], [], [V("wnr")])
+    for k in range(4):
+        dma("ys"[k % 2], "dos%d" % k, T.osc[4 * k:4 * k + 4, :], ap(V("zqs", 0, 128, 32 * k, 32 * k + 4)), [], [V("zqs")])
     finish()

from concourse.bass import DstId, RemoteDMATransfer
from concourse.mybir import dt, AluOpType, AxisListType, ActivationFunctionType

OP, ACT = AluOpType, ActivationFunctionType
CAPP, CAPR = 48, 32
LEAST = 128
Z0 = LEAST - CAPP
END = Z0 + 8 * CAPP
FW = 144
CUT = 96
TW = 160
BIG = 9e29
BANK = 512
UNIT = 1024.0
BATCH = ((0, 3), (3, 3), (6, 2))

SCRATCH = {"ps": ("psum", [128, 8 * BANK], "float32"), "f0": ("sbuf", [32, 128], "bfloat16"),
           "zb": ("sbuf", [32, 128], "bfloat16"), "lt": ("sbuf", [32, 32], "float32"), "fr": ("sbuf", [32, 192], "bfloat16")}
for _n, _w in (("off", 32), ("poff", 4), ("loff", 32), ("zoff", 16), ("toff", 16), ("aboff", 8), ("soff", 6), ("noff", 2), ("roff", 2)):
    SCRATCH[_n] = ("sbuf", [128, _w], "uint16")
for _n, _w in (("xt", 512), ("rtt", 544), ("wt", 2048), ("ut", 8), ("ur", 512), ("vt", 512), ("n4", 32),
               ("ht", 4 * END), ("cb", 128), ("tmp", 256), ("tms", 256), ("zw", TW), ("tr", 32), ("bi", 64), ("bt", 64), ("se", 32),
               ("rk", TW), ("nm", FW), ("ct", FW), ("ov", FW), ("role", FW), ("ma", FW), ("dd", FW), ("lim", 3 * FW), ("seg2", TW),
               ("cin", 1), ("d0", 64), ("cp", 64), ("sg", 64), ("seg", TW)):
    SCRATCH[_n] = ("sbuf", [128, _w], "bfloat16")
for _n, _w in (("tri", 3 * FW), ("va", TW), ("ta", TW), ("val", 3 * TW), ("tv", TW)):
    SCRATCH[_n] = ("sbuf", [128, _w], "float16")
for _n, _w in (("xq", 2 * LEAST), ("rq", 128), ("rp", 128), ("wq", 512), ("uq", 128), ("vq", 128), ("xd", 512),
               ("xf", LEAST + 2), ("xr", END), ("hq0", 144), ("hq1", 144), ("hq2", 144), ("hr", END), ("zq", 128)):
    SCRATCH[_n] = ("sbuf", [128, _w], "float8_e4m3fn_x4")
    SCRATCH[_n + "s"] = ("sbuf", [128, _w], "uint8")
for _n, _w in (("ci", 288), ("cc", 288), ("c2", 4), ("bc", 1), ("sc", 1), ("c8", 32), ("s8", TW),
               ("thr", 32), ("bs", 64), ("lc", 4), ("of", 32), ("lab", TW), ("tab", 2 * END),
               ("qw", END), ("yw", END), ("ga", FW), ("gb", FW), ("wnr", 16), ("ysb", 128)):
    SCRATCH[_n] = ("sbuf", [128, _w], "float32")
DMAS = ["dx", "drt", "dw0", "dw1", "du", "dv", "doc", "dos0", "dos1", "dos2", "dos3", "dy", "dwn"]
SEMAPHORES = ["cv", "cs", "ct", "cg", "ls", "xf", "xl", "xa0", "xa1", "xa2", "ha0", "ha1", "ha2"] + DMAS


def _runner(g, T):
    queues = {"v": g.vector, "s": g.scalar, "t": g.tensor, "g": g, "y": g.sync}
    own = {"v": "cv", "s": "cs", "t": "ct", "g": "cg"}
    total, known, snap, recs = {}, {q: {} for q in queues}, {}, {}

    def region(view):
        b, p0, p1, c0, c1, st = view
        if SCRATCH[b][0] == "psum":
            return (0, 128, c0 // BANK * BANK, -(-c1 // BANK) * BANK, 1)
        return (p0, p1, c0, c1, st)

    def meet(a, b):
        if a[0] >= b[1] or b[0] >= a[1] or a[2] >= b[3] or b[2] >= a[3]:
            return False
        return not (a[4] > 1 and a[4] == b[4] and (a[2] - b[2]) % a[4])

    def wait_for(q, need):
        need = [(s, v) for s, v in need.items() if known[q].get(s, 0) < v]
        for i, (s, v) in enumerate(need):
            if any(snap.get(o, {}).get(s, 0) >= v for j, o in enumerate(need) if j != i):
                continue
            queues[q].wait_ge(T.sem[s], v)
        for s, v in need:
            known[q][s] = max(known[q].get(s, 0), v)
            for s2, v2 in snap.get((s, v), {}).items():
                known[q][s2] = max(known[q].get(s2, 0), v2)

    def wants(q, outs, ins):
        need = {}
        for wr, views in ((True, outs), (False, ins)):
            for view in views:
                r = region(view)
                ps = SCRATCH[view[0]][0] == "psum"
                for w, r2, tok, q2 in recs.get(view[0], []):
                    if not (wr or w or (ps and q2 != q)) or not meet(r, r2):
                        continue
                    need[tok[0]] = max(need.get(tok[0], 0), tok[1])
        return need

    def note(q, outs, ins, tok):
        for wr, views in ((True, outs), (False, ins)):
            for view in views:
                recs.setdefault(view[0], []).append((wr, region(view), tok, q))

    def op(q, call, outs, ins, dma=None):
        wait_for(q, wants(q, outs, ins))
        sem, n = (dma, 16) if dma else (own[q], 1)
        call(queues[q]).then_inc(T.sem[sem], n)
        total[sem] = total.get(sem, 0) + n
        tok = (sem, total[sem])
        snap[tok] = dict(known[q])
        note(q, outs, ins, tok)

    def arrive(sem, n, outs):
        total[sem] = total.get(sem, 0) + n
        note("far", outs, [], (sem, total[sem]))

    def send(call, ins, ls):
        wait_for("g", wants("g", [], ins))
        call(g)
        total["ls"] = total.get("ls", 0) + ls

    def finish():
        wait_for("g", dict(total))

    return op, arrive, send, finish


def rank_program(g, core, T, topo):
    rank = T.rank_of(core)
    if rank is None:
        return
    op, arrive, send, finish = _runner(g, T)
    N = len(T.cores)

    def kind(i):
        c = T.cores[rank ^ i]
        return (topo.chip(c) == topo.chip(core), topo.die(c) == topo.die(core))

    peer = [i for i in range(1, N) if kind(i)[0]]
    same = [i for i in range(1, N) if kind(i) == (False, True)]
    other = [i for i in range(1, N) if kind(i) == (False, False)]
    order = [0, same[0], other[0], peer[0], other[1], same[1], other[2], same[2]]

    def who(p):
        return rank ^ order[p]

    place = [order.index(e ^ rank) for e in range(N)]
    batch = [(list(range(p0, p0 + n)), Z0 + CAPP * p0, Z0 + CAPP * (p0 + n)) for p0, n in BATCH]
    sent = [[p for p in bt[0] if p > 1] for bt in batch]
    back = [[p for p in bt[0] if p > 0] for bt in batch]
    away = topo.engines(core, T.cores[who(1)])
    near = [e for e in topo.engines(core, T.cores[rank ^ peer[0]]) if e not in away][:len(away) // 2]

    def bits(es):
        return sum(1 << e for e in es)

    def V(b, c0=0, c1=None, p0=0, p1=None, st=1):
        sh = SCRATCH[b][1]
        return (b, p0, sh[0] if p1 is None else p1, c0, sh[1] if c1 is None else c1, st)

    def ap(v):
        b, p0, p1, c0, c1, st = v
        return T[b][p0:p1, c0:c1] if st == 1 else T[b][p0:p1, c0:c1:st]

    def by(v):
        return ap(v).bitcast(dt.uint8)

    def zeros(n, p0=0, p1=128):
        return V("rtt", 4 * N, 4 * N + n, p0, p1)

    def tri(j, a=0, b=FW):
        return V("tri", 3 * a + j, 3 * b, st=3)

    def memset(v, x):
        op("v", lambda q: q.memset(ap(v), x), [v], [])

    def act(out, in_, f, lst=None, acc=None, **k):
        src = ap(in_) if lst is None else ap(in_).indirect(ap(lst))
        cols = [x for x in k.values() if isinstance(x, tuple)]
        kk = {n: ap(x) if isinstance(x, tuple) else x for n, x in k.items()}
        if acc is not None:
            kk["accum_out"] = ap(acc)
        op("s", lambda q: q.activation(ap(out), src, f, **kk), [out] + ([acc] if acc else []),
           [in_] + cols + ([lst] if lst else []))

    def fill(v, x):
        act(v, zeros(len(range(v[3], v[4], v[5])), v[1], v[2]), ACT.Identity, bias=x)

    def copy(out, in_, q="v", lst=None):
        if q == "v":
            src = ap(in_) if lst is None else ap(in_).indirect(ap(lst))
            op("v", lambda e: e.tensor_copy(ap(out), src), [out], [in_] + ([lst] if lst else []))
        else:
            act(out, in_, ACT.Copy, lst)

    def tt(out, a, b, o, lst=None):
        src = ap(a) if lst is None else ap(a).indirect(ap(lst))
        op("v", lambda q: q.tensor_tensor(ap(out), src, ap(b), o), [out], [a, b] + ([lst] if lst else []))

    def ts(out, a, s1, o1, s2=None, o2=None, lst=None):
        ins = [a] + [s for s in (s1, s2, lst) if isinstance(s, tuple)]
        src = ap(a) if lst is None else ap(a).indirect(ap(lst))
        x1, x2 = (ap(s) if isinstance(s, tuple) else s for s in (s1, s2))
        if o2 is None:
            op("v", lambda q: q.tensor_scalar(ap(out), src, x1, None, o1), [out], ins)
        else:
            op("v", lambda q: q.tensor_scalar(ap(out), src, x1, x2, o1, o2), [out], ins)

    def total(out, in_):
        op("v", lambda e: e.tensor_reduce(ap(out), ap(in_), AxisListType.X, OP.add), [out], [in_])

    def scan(out, a, b, init=0.0, o0=OP.add, o1=OP.add):
        ini = ap(init) if isinstance(init, tuple) else init
        op("v", lambda q: q.tensor_tensor_scan(ap(out), ap(a), ap(b), ini, o0, o1), [out],
           [a, b] + ([init] if isinstance(init, tuple) else []))

    def runs(out, mask, in_):
        scan(out, mask, in_, 0.0, OP.mult)

    def turn(out, in_):
        op("v", lambda q: q.transpose(ap(out), ap(in_)), [out], [in_])

    def quant(c, t, a=0, b=None, d=0):
        n = SCRATCH[t][1][1] // 4 if b is None else b - a
        o, s, i = V(c, d, d + n), V(c + "s", d, d + n), V(t, 4 * a, 4 * (a + n))
        op("v", lambda q: q.quantize_mx(ap(o), ap(s), ap(i)), [o, s], [i])

    def mm(bank, l, la, r, ra, rb):
        out, lc, ls, rc, rs = V("ps", BANK * bank, BANK * bank + rb - ra), V(l, la, la + 128), V(l + "s", la, la + 128), V(r, ra, rb), V(r + "s", ra, rb)
        op("t", lambda q: q.matmul_mx(ap(out), ap(lc), ap(ls), ap(rc), ap(rs), True, True), [out], [lc, ls, rc, rs])

    def pick(o, w, lst):
        op("v", lambda q: q.tensor_copy(ap(o).bitcast(dt.uint32), ap(w).bitcast(dt.uint32).indirect(ap(lst))), [o], [w, lst])

    def picks(dst, d, lst, src="xq"):
        n = 16 * (lst[4] - lst[3])
        pick(V(dst, d, d + n), V(src), lst)
        act(V(dst + "s", d, d + n), V(src + "s"), ACT.Copy, lst)

    def dma(q, sem, dst, src, outs, ins):
        op(q, lambda e: e.dma_start(dst, src), outs, ins, dma=sem)

    def iota(v, pattern, b, cm=0):
        op("g", lambda q: q.iota(ap(v), pattern, b, cm, allow_small_or_imprecise_dtypes=True), [v], [])

    def table(b, c0, vals, rep):
        for i in range(0, len(vals), 4):
            a = vals[i:i + 4]
            if a[3] - a[2] == a[1] - a[0]:
                iota(V(b, c0 + rep * i, c0 + rep * (i + 4)), [[a[2] - a[0], 2], [a[1] - a[0], 2], [0, rep]], a[0])
            else:
                for j in (0, 2):
                    iota(V(b, c0 + rep * (i + j), c0 + rep * (i + j + 2)), [[a[j + 1] - a[j], 2], [0, rep]], a[j])

    def transfer(p, eng, sem, src, dst):
        rid, pid, _s = topo.addr(T.cores[who(p)])
        return RemoteDMATransfer(dst_ids=[DstId(rid=rid, pnc=pid)], dma_engine_mask=bits(eng), remote_sem=T.sem[sem], src=src, dst=dst)

    def early(sem, s, d, f):
        send(lambda q: q.remote_dma_fused([transfer(1, away, sem, f(s), f(d))], local_sem=T.sem["ls"]), [s], len(away))

    def shares(places):
        far = [p for p in places if order[p] != peer[0]]
        k = len(away) // len(far)
        return [(p, away[k * far.index(p):k * far.index(p) + k] if p in far else near) for p in places]

    def ship(places, src, s0, dst, sem):
        for x, f in (("", by), ("s", ap)):
            trs, ins, ls = [], [], 0
            for p, eng in shares(places):
                a, d0 = s0(p), Z0 + CAPP * p
                s, d = V(src + x, a, a + CAPP), V(dst + x, d0, d0 + CAPP)
                trs.append(transfer(p, eng, sem, f(s), f(d)))
                ins.append(s)
                ls += len(eng)
            send(lambda q: q.remote_dma_fused(trs, local_sem=T.sem["ls"]), ins, ls)

    def land(places, dst, sem):
        arrive(sem, sum(2 * len(eng) for p, eng in shares(places)),
               [V(dst + x, Z0 + CAPP * p, Z0 + CAPP * p + CAPP) for p in places for x in ("", "s")])

    dma("s", "drt", ap(V("rtt", 0, 4 * N)), T.rt[:, 0:4 * N], [V("rtt", 0, 4 * N)], [])
    dma("y", "dx", ap(V("xt")), T.x[:, :], [V("xt")], [])
    dma("y", "du", ap(V("ut", 0, 4)), T.u[:, 0:4], [V("ut", 0, 4)], [])
    dma("y", "dw0", ap(V("wt", 0, 1024)), T.w[:, 0:1024], [V("wt", 0, 1024)], [])
    dma("y", "dw1", ap(V("wt", 1024, 2048)), T.w[:, 1024:2048], [V("wt", 1024, 2048)], [])
    dma("y", "dv", ap(V("vt")), T.v[:, :], [V("vt")], [])

    iota(V("ci", 0, 32), [[0, 4], [1, 8]], 0)
    iota(V("ci", 32, 64), [[0, 2], [1, 2], [0, 8]], 0)
    iota(V("c2"), [[2, 4]], 0)
    table("thr", 0, [N - 1 - who(p) for p in range(N)], 4)
    iota(V("bi", 0, 32), [[0, 8], [-16, 4]], 0, -4)
    iota(V("ci", 64, 96), [[0, 32]], 31, 1)
    iota(V("ci", 96, 128), [[0, 8], [1, 4]], 0)
    iota(V("ci", 128, 160), [[0, 2], [16, 16]], 7)
    iota(V("ci", 160, 192), [[-16, 2], [16, 16]], 23)
    ecol, hcol, qcol, mcol, gcol, lcol, pcol = (V("cc", c, c + 1) for c in (0, 32, 64, 96, 128, 160, 192))
    memset(zeros(512), 0.0)
    memset(V("d0"), 1.0)
    memset(V("d0", 9, 64, st=9), -1.0)
    memset(V("d0", 0, 64, st=8), 0.0)
    turn(V("cc", 0, 64), V("ci", 0, 64))
    ts(V("aboff", 0, 4), V("c2"), hcol, OP.add, ecol, OP.min)
    ts(V("aboff", 4, 8), V("c2"), hcol, OP.add, ecol, OP.max)
    fill(V("zb"), 0.0)
    copy(V("bi", 32, 64), V("ci", 32, 64), "s")
    for k in range(4):
        act(V("ci", 224 + 16 * k, 240 + 16 * k), V("thr", 16 * (k // 2), 16 * (k // 2) + 16), ACT.Identity, scale=-8.0, bias=63.0)
    quant("xq", "rtt", N, N + LEAST, LEAST)

    quant("rq", "rtt", 0, LEAST)
    ts(V("c8"), V("ci", 0, 32), -1.0, OP.mult, 8.0, OP.add)
    pick(V("rp"), V("rq"), V("aboff"))
    act(V("rps"), V("rqs"), ACT.Copy, V("aboff"))
    quant("xq", "xt", 0, LEAST)
    mm(0, "xq", 0, "rp", 0, 128)
    early("xf", V("xqs", 0, LEAST + 2), V("xfs"), ap)
    early("xf", V("xq", 0, LEAST + 2), V("xf"), by)
    fill(V("ht", 0, 4 * Z0), 0.0)
    turn(V("cc", 224, 288), V("ci", 224, 288))
    ts(V("roff"), V("cc", 0, 2), 8.0, OP.mult, 7.0, OP.add)
    turn(V("cc", 64, 192), V("ci", 64, 192))
    copy(V("bs"), V("ps", 64, 128))
    copy(V("noff"), V("cc", 224, 288, st=32))
    tt(V("cp"), V("ps", 0, 64), V("bs"), OP.is_ge)
    ts(V("bc"), mcol, 1.5, OP.is_ge, 64.0, OP.mult)
    runs(V("sg"), V("d0"), V("cp"))
    ts(V("sc"), V("bc"), -1.0 / 128, OP.mult, 1.0, OP.add)
    tt(V("n4"), V("sg"), V("thr"), OP.is_ge, V("noff"))
    copy(V("se"), V("sg"), "s", V("roff"))
    turn(V("bt"), V("bi"))
    for c0 in (0, 160):
        fill(V("fr", c0, c0 + 32), 8.0)
    fill(V("zw"), 0.0)
    for a in range(4):
        turn(V("f0", 32 * a, 32 * a + 32), V("n4", 0, 32, 32 * a, 32 * a + 32))
    fill(V("seg"), 1.0)
    fill(V("seg", 0, TW, st=8), 0.0)
    copy(V("va", FW, TW), zeros(TW - FW))
    for a in range(4):
        scan(V("cb", 0, 128, 32 * a, 32 * a + 32), V("f0"), V("zb"), V("bt", a, a + 1, 0, 32))
    copy(V("val", 3 * FW + 2, 3 * TW, st=3), zeros(TW - FW))
    for m in (2, 3):
        act(V("tms", 128 * m - 256, 128 * m - 128), V("cb"), ACT.Sign, acc=V("lc", m, m + 1), bias=m + 0.5, scale=-1.0)
    for m in (0, 1):
        ts(V("tmp", 128 * m, 128 * m + 128), V("cb"), float(m), OP.is_le)
    for m in (0, 1):
        total(V("lc", m, m + 1), V("tmp", 128 * m, 128 * m + 128))
    ts(V("soff", 0, 1), gcol, TW - 1.0, OP.min)
    for a in range(4):
        for d in (0, 16):
            copy(V("lt", d + 4 * a, d + 4 * a + 4), V("lc", 0, 4, 32 * a, 32 * a + 32), "s" if d else "v")
    ts(V("soff", 1, 2), gcol, 8.0, OP.add, TW - 1.0, OP.min)
    for a in range(2):
        turn(V("of", 0, 32, 32 * a, 32 * a + 32), V("lt"))
    ts(V("soff", 2, 3), lcol, TW - 1.0, OP.min)
    for a in range(2):
        ts(V("off", 0, 32, 64 * a, 64 * a + 64), V("of", 0, 32, 0, 64), V("sc", 0, 1, 0, 64), OP.mult, V("bc", 0, 1, 0, 64), OP.add)
    tt(V("tr"), V("c8"), V("se"), OP.subtract)

    early("xl", V("off", 4, 7), V("poff", 0, 3), ap)
    for h, to in enumerate(sent):
        picks("xd", 64 * to[0], V("off", 4 * to[0], 4 * to[-1] + 3))
        ship(to, "xd", lambda p: 64 * p, "xr", "xa%d" % h)
    picks("xr", Z0, V("off", 0, 3))
    copy(V("soff", 4, 5), qcol)
    table("ci", 192, [Z0 - 1 + CAPP * place[e] for e in range(N)], 1)

    quant("wq", "wt")
    arrive("xf", 2 * len(away), [V("xf"), V("xfs")])
    arrive("xl", len(away), [V("poff", 0, 3)])
    picks("xr", Z0 + CAPP, V("poff", 0, 3), "xf")
    for a in range(4):
        turn(V("fr", 32 + 32 * a, 64 + 32 * a), V("tr", 0, 32, 32 * a, 32 * a + 32))

    def ranks():
        for n, c in ((32, 32), (16, 16)):
            for a in range(2):
                copy(V("rk", 0, FW, 32 * a, 32 * a + n), V("fr", c, c + FW, 0, n))
        copy(V("rk", 0, FW, 64, 128), V("rk", 0, FW, 0, 64))
        for t in range(4):
            fill(V("ur", t, 512, st=4), V("ut", t, t + 1))

    def over():
        copy(V("ci", 200, 208), V("ci", 192, 200), "s")
        copy(V("ci", 208, 224), V("ci", 192, 208), "s")
        act(V("ov"), V("ct"), ACT.Relu, scale=2.0, bias=-2.0 * CAPP)

    gaps = {(0, 0): ranks, (0, 1): lambda: ts(V("nm"), V("rk", 0, FW), 1.0, OP.is_le),
            (0, 2): lambda: scan(V("ct"), V("nm"), V("zw", 0, FW)), (0, 3): over,
            (1, 0): lambda: quant("hr", "ht", 0, LEAST), (1, 1): lambda: turn(V("cc", 192, 224), V("ci", 192, 224)),
            (1, 2): lambda: ts(tri(1), V("ct"), pcol, OP.add, 1.0 / UNIT, OP.mult)}

    def gap(h, i):
        if (h, i) in gaps:
            gaps[h, i]()

    for h, (places, c0, c1) in enumerate(batch):
        w0 = min(c0, c1 - LEAST)
        land(sent[h], "xr", "xa%d" % h)
        banks = [4 * (h % 2) + i for i in range(4)]
        for i in (0, 2, 1, 3):
            mm(banks[i], "wq", 128 * i, "xr", w0, c1)
        for i in (0, 2, 1, 3):
            r, o = V("ps", BANK * banks[i] + c0 - w0, BANK * banks[i] + c1 - w0), V("ht", 4 * c0 + i, 4 * c1, st=4)
            if i < 2:
                gap(h, i)
                ts(o, r, 0.0, OP.max, 0.0625, OP.mult)
            else:
                act(o, r, ACT.Relu, scale=0.0625)
        gap(h, 2)
        q0 = min(max(c0, LEAST), c1 - LEAST)
        quant("hq%d" % h, "ht", q0, c1)
        ship(back[h], "hq%d" % h, lambda p: Z0 + CAPP * p - q0, "hr", "ha%d" % h)
        gap(h, 3)

    iota(V("tab", END - Z0, END + Z0 - 1), [[0, 2 * Z0 - 1]], -100)
    table("tab", END - 1 + Z0, [who(p) for p in range(N)], CAPP)
    table("tab", 0, [-1 - who(N - 1 - p) for p in range(N)], CAPP)

    half = V("bt", 32, 33)
    tt(V("role"), V("rk", 0, FW), V("ov"), OP.add)
    quant("uq", "ur")
    fill(V("qw", 0, Z0), -BIG)
    fill(V("yw", 0, Z0), 0.0)
    fill(V("lim"), 0.0)
    copy(V("seg2"), V("seg"), "s")
    act(V("cin"), half, ACT.Identity, scale=255.5 - CAPR, bias=CAPR + 0.5)
    fill(V("lim", 0, 3 * FW, st=3), UNIT)
    fill(V("seg2", 8, TW, st=16), -2.0)
    ts(V("ma"), V("role"), half, OP.is_equal)
    tt(V("va", 0, FW), V("ma"), tri(1), OP.mult)
    turn(V("ta"), V("va"))
    quant("vq", "vt")
    runs(V("lab"), V("seg"), V("ta"))
    ts(V("loff"), V("lab"), UNIT, OP.mult, lst=V("soff", 0, 2))

    last = len(batch) - 1
    cuts, blocks = ((0, CUT), (CUT, FW)), ((0, CUT), (CUT, TW))
    for h, (places, c0, c1) in enumerate(batch):
        w0 = min(c0, c1 - LEAST)
        land(back[h], "hr", "ha%d" % h)
        mm(h, "uq", 0, "hr", w0, c1)
        copy(V("qw", c0, c1), V("ps", BANK * h + c0 - w0, BANK * h + c1 - w0), "v" if h == last else "s")
    for a, b in cuts:
        copy(V("ga", a, b), V("qw"), "v", V("loff", a // 16, b // 16))
        copy(V("gb", a, b), V("qw"), "s", V("loff", 16 + a // 16, 16 + b // 16))
    for h, (places, c0, c1) in enumerate(batch):
        w0 = min(c0, c1 - LEAST)
        mm(4 + h, "vq", 0, "hr", w0, c1)
        copy(V("yw", c0, c1), V("ps", BANK * (4 + h) + c0 - w0, BANK * (4 + h) + c1 - w0), "s")
    for a, b in cuts:
        tt(V("dd", a, b), V("gb", a, b), V("ga", a, b), OP.is_gt)
    for a, b in cuts:
        tt(tri(2, a, b), V("dd", a, b), V("role", a, b), OP.is_equal)
    scan(tri(0), V("zw", 0, FW), tri(2), V("cin"), OP.add, OP.subtract)
    for a, b in cuts:
        scan(V("val", 3 * a, 3 * b), V("lim", 3 * a, 3 * b), V("tri", 3 * a, 3 * b), 0.0, OP.max, OP.min)
    for a, b in blocks:
        turn(V("tv", a, b), V("val", 3 * a + 2, 3 * b, st=3))
    for a, b in blocks:
        runs(V("s8", a, b), V("seg2", a, b), V("tv", a, b))
    z = V("zoff", 0, 8)
    ts(V("zoff"), V("s8"), UNIT, OP.mult, lst=V("soff", 2, 3))
    ts(V("toff"), V("s8"), -UNIT, OP.mult, float(END - 1), OP.add, lst=V("soff", 4, 5))
    pick(V("zq"), V("hr"), z)
    dma("y", "doc", T.oc[:, :], by(V("zq")), [], [V("zq")])
    act(V("ysb"), V("yw"), ACT.Copy, z)
    dma("y", "dy", T.y[:, :], ap(V("ysb")), [], [V("ysb")])
    copy(V("zqs"), V("hrs"), "v", z)
    act(V("wnr"), V("tab", 0, 2 * END - 1), ACT.Copy, V("toff", 0, 1))
    dma("s", "dwn", T.wn[:, :], T.wnr[0:128:16, 0:16], [], [V("wnr")])
    for k in range(4):
        dma("ys"[k % 2], "dos%d" % k, T.osc[4 * k:4 * k + 4, :], ap(V("zqs", 0, 128, 32 * k, 32 * k + 4)), [], [V("zqs")])
    finish()
